import numpy as np
import ml_dtypes


def mxq(x, axis, fmt="e4m3"):
    dtype, down = {"e4m3": (ml_dtypes.float8_e4m3fn, 7), "e5m2": (ml_dtypes.float8_e5m2, 14)}[fmt]
    v = np.moveaxis(np.asarray(x, np.float32).astype(ml_dtypes.bfloat16).astype(np.float64), axis, -1)
    blocks = v.reshape(v.shape[:-1] + (-1, 32))
    amax = np.abs(blocks).max(-1, keepdims=True)
    byte = np.maximum(np.where(amax > 0, np.frexp(amax)[1] - 1 + 127, 0) - down, 1)
    scale = np.exp2(byte - 127.0)
    codes = (blocks / scale).astype(np.float32).astype(dtype).astype(np.float64)
    return np.moveaxis((codes * scale).reshape(v.shape), -1, axis)


WIDE = False


def mx_kscale(k):
    if not WIDE:
        return np.ones(k)
    levels = np.array([10, -10, 5, -5, 0])
    if k % 512:
        return np.exp2(np.random.permutation(np.resize(levels, k // 32))).repeat(32)
    a = np.empty((k // 512, 16))
    for p in range(k // 512):
        a[p, :8] = np.random.permutation(np.resize(levels, 8))
        for g in range(8):
            far = levels[np.abs(levels - a[p, g]) >= 10]
            a[p, g + 8] = far[np.random.randint(len(far))]
    return np.exp2(a.ravel()).repeat(32)


BF16 = ml_dtypes.bfloat16


def bf(x):
    return np.asarray(x, np.float32).astype(BF16)


def f64(x):
    return np.asarray(x).astype(np.float64)


E2M1 = np.array([0.0, 0.5, 1.0, 1.5, 2.0, 3.0, 4.0, 6.0, -0.0, -0.5, -1.0, -1.5, -2.0, -3.0, -4.0, -6.0])


def pack_weight(w, fmt):
    k, n = w.shape
    w = f64(bf(w)).reshape(k // 32, 32, n)
    amax = np.abs(w).max(1)
    if fmt == "e4m3":
        byte = np.frexp(amax)[1] - 1 + 127 - 7
    else:
        mant, ex = np.frexp(amax / 6.0)
        byte = np.where(mant > 0.5, ex, ex - 1) + 127
    byte = np.clip(np.where(amax > 0, byte, 1), 1, 254)
    scaled = (w * np.exp2(127.0 - byte)[:, None, :]).reshape(k, n).astype(np.float32)
    by_word = np.ascontiguousarray(scaled.reshape(k // 512, 128, 4, n).transpose(0, 1, 3, 2))
    if fmt == "e4m3":
        words = by_word.astype(ml_dtypes.float8_e4m3fn).view(np.uint8)
    else:
        c = by_word.astype(ml_dtypes.float4_e2m1fn).view(np.uint8) & 0xF
        words = c[..., 0::2] | (c[..., 1::2] << 4)
    return np.ascontiguousarray(words), np.ascontiguousarray(byte.astype(np.uint8).reshape(k // 512, 16, n))


def unpack_weight(words, scales, fmt):
    g, p, n, _ = words.shape
    if fmt == "e4m3":
        vals = np.ascontiguousarray(words).view(ml_dtypes.float8_e4m3fn).astype(np.float64)
    else:
        nib = np.empty((g, p, n, 4), np.uint8)
        nib[..., 0::2] = words & 0xF
        nib[..., 1::2] = words >> 4
        vals = E2M1[nib]
    vals = vals * np.repeat(np.exp2(scales.astype(np.float64) - 127.0), 8, axis=1)[..., None]
    return vals.transpose(0, 1, 3, 2).reshape(g * 512, n)
def pack4(w):
    words, scales = pack_weight(w, "e2m1")
    return words.reshape(words.shape[0], 128, -1), scales


def unpack4(words, scales):
    return unpack_weight(words.reshape(words.shape[0], 128, -1, 2), scales, "e2m1")


P, K, F, D, L, C = 512, 1024, 1024, 1024, 8, 128


def draw0():
    s = mx_kscale(K)
    u = mx_kscale(D)
    t = mx_kscale(F)
    wkv = np.random.standard_normal((D, 2 * L * C)) / np.sqrt(D) / u[:, None]
    wkv_words, wkv_scales = pack4(wkv)
    return {
        "codes": bf(np.random.standard_normal((P, K)) * s),
        "w_in": bf(np.random.standard_normal((K, F)) / np.sqrt(K) / s[:, None]),
        "bias": bf(0.3 * np.random.standard_normal(F)),
        "gain": bf((1 + 0.1 * np.random.standard_normal(F)) * t),
        "w_up": bf(np.random.standard_normal((F, D)) / np.sqrt(np.sqrt(F)) * u / t[:, None]),
        "wkv_words": wkv_words,
        "wkv_scales": wkv_scales,
    }


def core(codes, w_in, bias, gain, w_up, wkv_words, wkv_scales):
    a = mxq(f64(codes), 1, "e4m3") @ mxq(f64(w_in), 0, "e4m3")
    h = np.tanh(a + f64(bias)) * f64(gain)
    w = unpack4(wkv_words, wkv_scales)
    m = mxq(f64(w_up), 1, "e4m3") @ w
    y = mxq(h, 1, "e4m3") @ mxq(m, 0, "e4m3")
    keys = y[:, :L * C]
    values = y[:, L * C:]
    return keys, values


def e4m3fn_bytes(y):
    return np.clip(np.asarray(y, np.float64), -448.0, 448.0).astype(np.float32).astype(ml_dtypes.float8_e4m3fn).view(np.uint8)


def e4m3fn_values(b):
    return np.asarray(b, np.uint8).view(ml_dtypes.float8_e4m3fn).astype(np.float64)


def setup_inputs():
    d = draw0()
    x0 = np.asarray(d['w_in']).astype(np.float64)
    s = (np.max(np.abs(x0), axis=(1,), keepdims=True) / 448.0).astype(np.float32)
    out = {}
    for k, v in d.items():
        if k == 'w_in':
            out['w_in_bytes'] = e4m3fn_bytes(x0 / s.astype(np.float64))
            out['w_in_scale'] = s
        else:
            out[k] = v
    return out


def reference(codes, w_in_bytes, w_in_scale, bias, gain, w_up, wkv_words, wkv_scales):
    return core(codes, e4m3fn_values(w_in_bytes) * w_in_scale.astype(np.float64), bias, gain, w_up, wkv_words, wkv_scales)

@@ -1,0 +1,371 @@
+from contextlib import ExitStack
+
+import concourse.mybir as mybir
+from concourse.masks import make_identity
+
+P = 128
+ROWS, K, F, D, N = 512, 1024, 1024, 1024, 2048
+FLOPS = 2 * (ROWS * K * F + F * D * N + ROWS * F * N)
+
+F32 = mybir.dt.float32
+BF16 = mybir.dt.bfloat16
+I32 = mybir.dt.int32
+U32 = mybir.dt.uint32
+U8 = mybir.dt.uint8
+FP8 = mybir.dt.float8_e4m3fn
+FP8X4 = mybir.dt.float8_e4m3fn_x4
+FP4X4 = mybir.dt.float4_e2m1fn_x4
+MULT = mybir.AluOpType.mult
+COPY = mybir.ActivationFunctionType.Copy
+TANH = mybir.ActivationFunctionType.Tanh
+
+
+def tile_prefix_tuning_kv_s11_kernel(
+    tc, codes, w_in_bytes, w_in_scale, bias, gain, w_up, wkv_words, wkv_scales, keys, values
+):
+    nc = tc.nc
+    with ExitStack() as ctx:
+        keep = ctx.enter_context(tc.tile_pool(name="keep", bufs=1))
+        wst = ctx.enter_context(tc.tile_pool(name="wst", bufs=8))
+        mst = ctx.enter_context(tc.tile_pool(name="mst", bufs=16))
+        yst = ctx.enter_context(tc.tile_pool(name="yst", bufs=12))
+        psum = ctx.enter_context(tc.psum_pool(name="psum", bufs=8))
+
+        ident = keep.tile([P, P], F32, name="ident")
+        make_identity(nc, ident[:])
+
+        wu_raw = [keep.tile([P, 4, D], BF16, name="wu_raw%d" % g, align_bytes=64) for g in range(2)]
+        wuq = [keep.tile([P, 4, 256], U32, name="wuq%d" % g, align_bytes=64) for g in range(2)]
+        wus = [keep.tile([P, 4, 256], U8, name="wus%d" % g, align_bytes=64) for g in range(2)]
+        cuts = (0, 512, 1024, N)
+        scuts = (0, 512, N)
+        w4, w4s = [], []
+        for i in range(3):
+            w4.append(keep.tile([P, 2, 2 * (cuts[i + 1] - cuts[i])], U8, name="w4_%d" % i, align_bytes=64))
+        for i in range(2):
+            w4s.append(keep.tile([P, 2, scuts[i + 1] - scuts[i]], U8, name="w4s_%d" % i, align_bytes=64))
+        craw = keep.tile([P, 4, K], BF16, name="craw", align_bytes=64)
+        cg = keep.tile([P, 2, ROWS, 4], BF16, name="cg", align_bytes=64)
+        cq = keep.tile([P, 2, ROWS], U32, name="cq", align_bytes=64)
+        cs = keep.tile([P, 2, ROWS], U8, name="cs", align_bytes=64)
+        wi = keep.tile([P, 2, 4, F], U8, name="wi", align_bytes=64)
+        wisc = keep.tile([P, 2, 4], F32, name="wisc")
+        wb = keep.tile([P, 2, 4, F], BF16, name="wb", align_bytes=64)
+        wg = keep.tile([P, 2, 2, 2048], BF16, name="wg", align_bytes=64)
+        wq = keep.tile([P, 2, 2, 512], U32, name="wq", align_bytes=64)
+        ws = keep.tile([P, 2, 2, 512], U8, name="ws", align_bytes=64)
+        bcol = keep.tile([P, 2, 4], BF16, name="bcol")
+        gcol = keep.tile([P, 2, 4], BF16, name="gcol")
+        th = [keep.tile([P, 4, ROWS], F32, name="th%d" % g, align_bytes=64) for g in range(2)]
+        hg = [keep.tile([P, ROWS, 4], BF16, name="hg%d" % g, align_bytes=64) for g in range(2)]
+        hq = [keep.tile([P, ROWS], U32, name="hq%d" % g, align_bytes=64) for g in range(2)]
+        hs = [keep.tile([P, ROWS], U8, name="hs%d" % g, align_bytes=64) for g in range(2)]
+        mq = [keep.tile([P, N], U32, name="mq%d" % g, align_bytes=64) for g in range(2)]
+        ms = [keep.tile([P, N], U8, name="ms%d" % g, align_bytes=64) for g in range(2)]
+        warm = keep.tile([P, 2], F32, name="warm")
+
+        ctx.enter_context(tc.manual_schedule())
+
+        zeros = keep.tile([P, 512], BF16, name="zeros", align_bytes=64)
+        nc.vector.memset(zeros[:], 0.0)
+        for i in range(2):
+            nc.vector.memset(w4s[i][:].rearrange("p a n -> p (a n)").bitcast(I32), 0)
+        nc.vector.memset(warm[:], 0.0)
+        nc.scalar.activation(out=warm[:, 1:2], in_=warm[:, 0:1], func=TANH)
+
+        wu_src = w_up.rearrange("(g p t) d -> g p t d", p=P, t=4)
+
+        def load_wu(g, t0, t1):
+            nc.sync.dma_start(out=wu_raw[g][:, t0:t1, :], in_=wu_src[g][:, t0:t1, :])
+
+        def load_w4(i):
+            nc.sync.dma_start(
+                out=w4[i][:].bitcast(I32),
+                in_=wkv_words.rearrange("g p b -> p g b")[:, :, 2 * cuts[i] : 2 * cuts[i + 1]].bitcast(I32),
+            )
+
+        def load_w4s(i):
+            for q in range(4):
+                nc.sync.dma_start(
+                    out=w4s[i][32 * q : 32 * q + 4, :, :].bitcast(I32),
+                    in_=wkv_scales[:, 4 * q : 4 * q + 4, scuts[i] : scuts[i + 1]]
+                    .rearrange("g r n -> r g n")
+                    .bitcast(I32),
+                )
+
+        load_wu(0, 0, 1)
+        load_w4s(0)
+        load_wu(0, 1, 2)
+        load_wu(0, 2, 3)
+        load_wu(0, 3, 4)
+        load_w4(0)
+        wi_src = w_in_bytes.rearrange("(g p t) f -> g p t f", p=P, t=4)
+        nc.sync.dma_start(out=wisc[:], in_=w_in_scale.rearrange("(g p t) o -> p g (t o)", p=P, t=4))
+        for h in range(2):
+            nc.sync.dma_start(out=wi[:, 0, 2 * h : 2 * h + 2, :], in_=wi_src[0][:, 2 * h : 2 * h + 2, :])
+        load_w4(1)
+        load_w4s(1)
+        nc.sync.dma_start(out=wi[:, 1], in_=wi_src[1])
+        c_src = codes.rearrange("(r p) k -> p r k", p=P)
+        for h in range(2):
+            nc.sync.dma_start(out=craw[:, 2 * h : 2 * h + 2, :], in_=c_src[:, 2 * h : 2 * h + 2, :])
+        load_w4(2)
+        load_wu(1, 0, 2)
+        load_wu(1, 2, 4)
+        nc.sync.dma_start(out=bcol[:], in_=bias.rearrange("(g p t) -> p g t", p=P, t=4))
+        nc.sync.dma_start(out=gcol[:], in_=gain.rearrange("(g p t) -> p g t", p=P, t=4))
+
+        def copy_out(eng, out, in_):
+            if eng == "S":
+                nc.scalar.copy(out=out, in_=in_)
+            else:
+                nc.vector.tensor_copy(out=out, in_=in_)
+
+        def bank():
+            b = psum.tile([P, 512], F32, name="bank", tag="bank")
+            return b
+
+        def turn(words):
+            b = bank()
+            for a in range(2):
+                for u in range(2):
+                    i = 2 * a + u
+                    nc.tensor.transpose(
+                        b[:, 128 * i : 128 * i + 128],
+                        words[:, 256 * a + u : 256 * (a + 1) : 2],
+                        ident[:],
+                    )
+            return b
+
+        banks = {}
+        wux = {}
+
+        def drain_wu(g, t, b, eng):
+            x = wst.tile([P, 2, 128, 4], BF16, name="wux", tag="wux", align_bytes=64)
+            wux[(g, t)] = x
+            copy_out(eng, x[:].bitcast(F32), b[:].rearrange("p (a u r) -> p a r u", a=2, u=2))
+
+        def quant_wu(g, t):
+            x = wux[(g, t)]
+            nc.vector.quantize_mx(
+                out=wuq[g][:, t, :].bitcast(FP8X4),
+                scales=wus[g][:, t, :],
+                in_=x[:].rearrange("p a r j -> p (a r j)"),
+            )
+
+        def drain_c(r, b, eng):
+            copy_out(
+                eng,
+                cg[:, :, 128 * r : 128 * r + 128, :].bitcast(F32),
+                b[:].rearrange("p (a u r) -> p a r u", a=2, u=2),
+            )
+
+        def quant_c(g):
+            nc.vector.quantize_mx(
+                out=cq[:, g, :].bitcast(FP8X4), scales=cs[:, g, :], in_=cg[:, g].rearrange("p n j -> p (n j)")
+            )
+
+        def widen(g, t, eng="V"):
+            if eng == "S":
+                nc.scalar.activation(
+                    out=wb[:, g, t, :], in_=wi[:, g, t, :].bitcast(FP8), func=COPY, scale=wisc[:, g, t : t + 1]
+                )
+                return
+            nc.vector.tensor_scalar(
+                out=wb[:, g, t, :],
+                in0=wi[:, g, t, :].bitcast(FP8),
+                scalar1=wisc[:, g, t : t + 1],
+                scalar2=None,
+                op0=MULT,
+            )
+
+        def lace(g, h):
+            nc.vector.tensor_copy(
+                out=wg[:, g, h, :].rearrange("p (t m j) -> p t m j", t=4, j=4),
+                in_=wb[:, g, :, 512 * h : 512 * h + 512].rearrange("p j (m t) -> p t m j", t=4),
+            )
+
+        def quant_wi(g, h):
+            nc.vector.quantize_mx(
+                out=wq[:, g, h, :].bitcast(FP8X4), scales=ws[:, g, h, :], in_=wg[:, g, h, :]
+            )
+
+        mx_tiles = {}
+
+        def unit_part(g, c, b, ts):
+            i = min(c // 4, 2)
+            n = 128 * c - cuts[i]
+            j = min(c // 4, 1)
+            m = 128 * c - scuts[j]
+            for t in ts:
+                for a in range(2):
+                    nc.tensor.matmul_mx(
+                        out=b[:, 128 * t : 128 * t + 128],
+                        lhsT=wuq[g][:, t, 128 * a : 128 * a + 128].bitcast(FP8X4),
+                        lhsT_scale=wus[g][:, t, 128 * a : 128 * a + 128],
+                        rhs=w4[i][:, a, 2 * n : 2 * n + 256].bitcast(FP4X4),
+                        rhs_scale=w4s[j][:, a, m : m + 128],
+                        start=(a == 0),
+                        stop=(a == 1),
+                    )
+            return b
+
+        def unit(g, c):
+            if g == 0 and c < 4:
+                if c == 0:
+                    for i in range(4):
+                        banks["U00%d" % i] = bank()
+                for i in range(4):
+                    unit_part(0, i, banks["U00%d" % i], [c])
+                return banks["U00%d" % c]
+            return unit_part(g, c, bank(), range(4))
+
+        def drain_m(g, c, b, eng):
+            if (g, c // 2) not in mx_tiles:
+                x = mst.tile([P, 2, 128, 4], BF16, name="mx", tag="mx", align_bytes=64)
+                mx_tiles[(g, c // 2)] = x
+            x = mx_tiles[(g, c // 2)]
+            copy_out(eng, x[:, c % 2], b[:].rearrange("p (t n) -> p n t", t=4))
+
+        def quant_m(g, d):
+            x = mx_tiles[(g, d)]
+            nc.vector.quantize_mx(
+                out=mq[g][:, 256 * d : 256 * d + 256].bitcast(FP8X4),
+                scales=ms[g][:, 256 * d : 256 * d + 256],
+                in_=x[:].rearrange("p i n j -> p (i n j)"),
+            )
+
+        def hidden(h, t):
+            b = bank()
+            for g in range(2):
+                nc.tensor.matmul_mx(
+                    out=b[:],
+                    lhsT=wq[:, g, h, 128 * t : 128 * t + 128].bitcast(FP8X4),
+                    lhsT_scale=ws[:, g, h, 128 * t : 128 * t + 128],
+                    rhs=cq[:, g, :].bitcast(FP8X4),
+                    rhs_scale=cs[:, g, :],
+                    start=(g == 0),
+                    stop=(g == 1),
+                )
+            return b
+
+        def drain_h(h, t, b):
+            nc.scalar.activation(out=th[h][:, t, :], in_=b[:], func=TANH, bias=bcol[:, h, t : t + 1])
+
+        def gains(h):
+            nc.vector.tensor_tensor(
+                out=hg[h][:],
+                in0=th[h][:].rearrange("p t n -> p n t"),
+                in1=gcol[:, h, :].unsqueeze(1).to_broadcast([P, ROWS, 4]),
+                op=MULT,
+            )
+
+        def quant_h(h):
+            nc.vector.quantize_mx(
+                out=hq[h][:].bitcast(FP8X4), scales=hs[h][:], in_=hg[h][:].rearrange("p n j -> p (n j)")
+            )
+
+        def final(i, c):
+            b = bank()
+            for g in range(2):
+                nc.tensor.matmul_mx(
+                    out=b[:],
+                    lhsT=hq[g][:, 128 * i : 128 * i + 128].bitcast(FP8X4),
+                    lhsT_scale=hs[g][:, 128 * i : 128 * i + 128],
+                    rhs=mq[g][:, 512 * c : 512 * c + 512].bitcast(FP8X4),
+                    rhs_scale=ms[g][:, 512 * c : 512 * c + 512],
+                    start=(g == 0),
+                    stop=(g == 1),
+                )
+            return b
+
+        def drain_y(i, c, b, eng):
+            y = yst.tile([P, 512], F32, name="y", tag="y", align_bytes=64)
+            dst = (keys if c < 2 else values)[128 * i : 128 * i + 128, 512 * (c % 2) : 512 * (c % 2) + 512]
+            parts = ((0, 512, eng),) if eng in "SV" else ((0, 256, "V"), (256, 512, "S"))
+            for n0, n1, e in parts:
+                copy_out(e, y[:, n0:n1], b[:, n0:n1])
+                nc.sync.dma_start(out=dst[:, n0:n1], in_=y[:, n0:n1])
+
+
+        def units(g, c0, c1, engs):
+            for c in range(c0, c1):
+                drain_m(g, c, unit_part(g, c, bank(), range(4)), engs[c % len(engs)])
+
+        def hiddens(h):
+            for t in range(4):
+                drain_h(h, t, hidden(h, t))
+
+        def finals(c, engs):
+            for i in range(4):
+                drain_y(i, c, final(i, c), engs[i])
+
+        d = bank()
+        for i in range(3):
+            nc.tensor.matmul(d[:], lhsT=zeros[:, 0:128], rhs=zeros[:], start=True, stop=True)
+
+        for t in range(4):
+            drain_wu(0, t, turn(wu_raw[0][:, t, :].bitcast(F32)), "SSVS"[t])
+            if t > 0:
+                quant_wu(0, t - 1)
+        quant_wu(0, 3)
+        first = []
+        for c in range(4):
+            b = bank()
+            first.append(b)
+        for t in range(4):
+            for c in range(4):
+                unit_part(0, c, first[c], [t])
+        for c in range(4):
+            drain_m(0, c, first[c], "S")
+        for g in range(2):
+            for t in range(4):
+                widen(g, t)
+        units(0, 4, 8, "S")
+        for r in range(4):
+            drain_c(r, turn(craw[:, r, :].bitcast(F32)), "S")
+        for g in range(2):
+            lace(g, 0)
+        for g in range(2):
+            quant_wi(g, 0)
+        for g in range(2):
+            quant_c(g)
+        units(0, 8, 12, "S")
+        for t in range(4):
+            drain_wu(1, t, turn(wu_raw[1][:, t, :].bitcast(F32)), "S")
+        for g in range(2):
+            lace(g, 1)
+        for t in range(4):
+            quant_wu(1, t)
+        for g in range(2):
+            quant_wi(g, 1)
+        units(0, 12, 16, "S")
+        hiddens(0)
+        units(1, 0, 4, "S")
+        hiddens(1)
+        quant_m(0, 0)
+        gains(0)
+        quant_m(0, 1)
+        quant_h(0)
+        quant_m(1, 0)
+        quant_m(1, 1)
+        gains(1)
+        quant_m(0, 2)
+        quant_h(1)
+        units(1, 4, 12, "S")
+        quant_m(0, 3)
+        for d in (2, 3):
+            quant_m(1, d)
+        for g in range(2):
+            for d in (4, 5):
+                quant_m(g, d)
+        finals(0, "SSVS")
+        for d in (6, 7):
+            quant_m(0, d)
+        finals(1, "SVSV")
+        units(1, 12, 14, "SV")
+        quant_m(1, 6)
+        units(1, 14, 16, "SV")
+        quant_m(1, 7)
+        finals(2, "SVSV")
+        finals(3, "SVS2")

@@ -181,8 +181,8 @@ def tile_prefix_tuning_kv_s11_kernel(
 
         def lace(g, h):
             nc.vector.tensor_copy(
-                out=wg[:, g, h, :].rearrange("p (t m j) -> p t m j", t=4, j=4),
-                in_=wb[:, g, :, 512 * h : 512 * h + 512].rearrange("p j (m t) -> p t m j", t=4),
+                out=wg[:, g, h, :].rearrange("p (t m j) -> p m j t", t=4, j=4),
+                in_=wb[:, g, :, 512 * h : 512 * h + 512].rearrange("p j (m t) -> p m j t", t=4),
             )
 
         def quant_wi(g, h):
@@ -254,9 +254,9 @@ def tile_prefix_tuning_kv_s11_kernel(
 
         def gains(h):
             nc.vector.tensor_tensor(
-                out=hg[h][:],
-                in0=th[h][:].rearrange("p t n -> p n t"),
-                in1=gcol[:, h, :].unsqueeze(1).to_broadcast([P, ROWS, 4]),
+                out=hg[h][:].rearrange("p (c i) t -> p c t i", i=2),
+                in0=th[h][:].rearrange("p t (c i) -> p c t i", i=2),
+                in1=gcol[:, h, :].unsqueeze(1).unsqueeze(3).to_broadcast([P, ROWS // 2, 4, 2]),
                 op=MULT,
             )
 

@@ -5,6 +5,7 @@ from concourse.masks import make_identity
 
 P = 128
 ROWS, K, F, D, N = 512, 1024, 1024, 1024, 2048
+HALF = ROWS // 2
 FLOPS = 2 * (ROWS * K * F + F * D * N + ROWS * F * N)
 
 F32 = mybir.dt.float32
@@ -26,62 +27,63 @@ def tile_prefix_tuning_kv_s11_kernel(
     nc = tc.nc
     with ExitStack() as ctx:
         keep = ctx.enter_context(tc.tile_pool(name="keep", bufs=1))
-        wst = ctx.enter_context(tc.tile_pool(name="wst", bufs=8))
-        mst = ctx.enter_context(tc.tile_pool(name="mst", bufs=16))
         yst = ctx.enter_context(tc.tile_pool(name="yst", bufs=12))
         psum = ctx.enter_context(tc.psum_pool(name="psum", bufs=8))
 
-        ident = keep.tile([P, P], F32, name="ident")
+        def sb(name, shape, dtype):
+            return keep.tile(shape, dtype, name=name, align_bytes=64)
+
+        ident = sb("ident", [P, P], F32)
         make_identity(nc, ident[:])
 
-        wu_raw = [keep.tile([P, 4, D], BF16, name="wu_raw%d" % g, align_bytes=64) for g in range(2)]
-        wuq = [keep.tile([P, 4, 256], U32, name="wuq%d" % g, align_bytes=64) for g in range(2)]
-        wus = [keep.tile([P, 4, 256], U8, name="wus%d" % g, align_bytes=64) for g in range(2)]
-        cuts = (0, 512, 1024, N)
+        wu_raw = [[sb("wu_raw%d%d" % (g, t), [P, D], BF16) for t in range(4)] for g in range(2)]
+        wux = [[sb("wux%d%d" % (g, t), [P, 2, 128, 4], BF16) for t in range(4)] for g in range(2)]
+        wuq = [sb("wuq%d" % g, [P, 4, 256], U32) for g in range(2)]
+        wus = [sb("wus%d" % g, [P, 4, 256], U8) for g in range(2)]
+        w4 = [sb("w4_%d" % c, [P, 2, 1024], U8) for c in range(4)]
         scuts = (0, 512, N)
-        w4, w4s = [], []
-        for i in range(3):
-            w4.append(keep.tile([P, 2, 2 * (cuts[i + 1] - cuts[i])], U8, name="w4_%d" % i, align_bytes=64))
-        for i in range(2):
-            w4s.append(keep.tile([P, 2, scuts[i + 1] - scuts[i]], U8, name="w4s_%d" % i, align_bytes=64))
-        craw = keep.tile([P, 4, K], BF16, name="craw", align_bytes=64)
-        cg = keep.tile([P, 2, ROWS, 4], BF16, name="cg", align_bytes=64)
-        cq = keep.tile([P, 2, ROWS], U32, name="cq", align_bytes=64)
-        cs = keep.tile([P, 2, ROWS], U8, name="cs", align_bytes=64)
-        wi = keep.tile([P, 2, 4, F], U8, name="wi", align_bytes=64)
-        wisc = keep.tile([P, 2, 4], F32, name="wisc")
-        wb = keep.tile([P, 2, 4, F], BF16, name="wb", align_bytes=64)
-        wg = keep.tile([P, 2, 2, 2048], BF16, name="wg", align_bytes=64)
-        wq = keep.tile([P, 2, 2, 512], U32, name="wq", align_bytes=64)
-        ws = keep.tile([P, 2, 2, 512], U8, name="ws", align_bytes=64)
-        bcol = keep.tile([P, 2, 4], BF16, name="bcol")
-        gcol = keep.tile([P, 2, 4], BF16, name="gcol")
-        th = [keep.tile([P, 4, ROWS], F32, name="th%d" % g, align_bytes=64) for g in range(2)]
-        hg = [keep.tile([P, ROWS, 4], BF16, name="hg%d" % g, align_bytes=64) for g in range(2)]
-        hq = [keep.tile([P, ROWS], U32, name="hq%d" % g, align_bytes=64) for g in range(2)]
-        hs = [keep.tile([P, ROWS], U8, name="hs%d" % g, align_bytes=64) for g in range(2)]
-        mq = [keep.tile([P, N], U32, name="mq%d" % g, align_bytes=64) for g in range(2)]
-        ms = [keep.tile([P, N], U8, name="ms%d" % g, align_bytes=64) for g in range(2)]
-        warm = keep.tile([P, 2], F32, name="warm")
+        w4s = [sb("w4s_%d" % i, [P, 2, scuts[i + 1] - scuts[i]], U8) for i in range(2)]
+        craw = [sb("craw%d" % r, [P, K], BF16) for r in range(4)]
+        cg = [sb("cg%d" % s, [P, 2, HALF, 4], BF16) for s in range(2)]
+        cq = [sb("cq%d" % s, [P, 2, HALF], U32) for s in range(2)]
+        cs = [sb("cs%d" % s, [P, 2, HALF], U8) for s in range(2)]
+        wi = [sb("wi%d" % g, [P, 4, F], U8) for g in range(2)]
+        wisc = sb("wisc", [P, 2, 4], F32)
+        wb = [sb("wb%d" % g, [P, 4, F], BF16) for g in range(2)]
+        wg = sb("wg", [P, 2, 2, 2048], BF16)
+        wq = sb("wq", [P, 2, 2, 512], U32)
+        ws = sb("ws", [P, 2, 2, 512], U8)
+        bcol = sb("bcol", [P, 2, 4], BF16)
+        gcol = sb("gcol", [P, 2, 4], BF16)
+        th = [[sb("th%d%d" % (s, g), [P, 4, HALF], F32) for g in range(2)] for s in range(2)]
+        hg = [sb("hg%d" % s, [P, 2, HALF, 4], BF16) for s in range(2)]
+        hq = [sb("hq%d" % s, [P, 2, HALF], U32) for s in range(2)]
+        hs = [sb("hs%d" % s, [P, 2, HALF], U8) for s in range(2)]
+        mx = [[sb("mx%d%d" % (g, c), [P, 4, 128, 4], BF16) for c in range(4)] for g in range(2)]
+        mq = [sb("mq%d" % g, [P, N], U32) for g in range(2)]
+        ms = [sb("ms%d" % g, [P, N], U8) for g in range(2)]
+        warm = sb("warm", [P, 2], F32)
+        zeros = sb("zeros", [P, 512], BF16)
 
         ctx.enter_context(tc.manual_schedule())
 
-        zeros = keep.tile([P, 512], BF16, name="zeros", align_bytes=64)
-        nc.vector.memset(zeros[:], 0.0)
-        for i in range(2):
-            nc.vector.memset(w4s[i][:].rearrange("p a n -> p (a n)").bitcast(I32), 0)
-        nc.vector.memset(warm[:], 0.0)
-        nc.scalar.activation(out=warm[:, 1:2], in_=warm[:, 0:1], func=TANH)
+        wu_src = w_up.rearrange("(g p t) d -> g t p d", p=P, t=4)
+        wi_src = w_in_bytes.rearrange("(g p t) f -> g p t f", p=P, t=4)
+        c_src = codes.rearrange("(r p) k -> r p k", p=P)
 
-        wu_src = w_up.rearrange("(g p t) d -> g p t d", p=P, t=4)
+        def load_wu(g, t):
+            nc.sync.dma_start(out=wu_raw[g][t][:], in_=wu_src[g][t])
 
-        def load_wu(g, t0, t1):
-            nc.sync.dma_start(out=wu_raw[g][:, t0:t1, :], in_=wu_src[g][:, t0:t1, :])
+        def load_c(r):
+            nc.sync.dma_start(out=craw[r][:], in_=c_src[r])
 
-        def load_w4(i):
+        def load_wi(g, t0, t1):
+            nc.sync.dma_start(out=wi[g][:, t0:t1, :], in_=wi_src[g][:, t0:t1, :])
+
+        def load_w4(c):
             nc.sync.dma_start(
-                out=w4[i][:].bitcast(I32),
-                in_=wkv_words.rearrange("g p b -> p g b")[:, :, 2 * cuts[i] : 2 * cuts[i + 1]].bitcast(I32),
+                out=w4[c][:].bitcast(I32),
+                in_=wkv_words.rearrange("g p b -> p g b")[:, :, 1024 * c : 1024 * c + 1024].bitcast(I32),
             )
 
         def load_w4s(i):
@@ -92,28 +94,6 @@ def tile_prefix_tuning_kv_s11_kernel(
                     .rearrange("g r n -> r g n")
                     .bitcast(I32),
                 )
-
-        load_wu(0, 0, 1)
-        load_w4s(0)
-        load_wu(0, 1, 2)
-        load_wu(0, 2, 3)
-        load_wu(0, 3, 4)
-        load_w4(0)
-        wi_src = w_in_bytes.rearrange("(g p t) f -> g p t f", p=P, t=4)
-        nc.sync.dma_start(out=wisc[:], in_=w_in_scale.rearrange("(g p t) o -> p g (t o)", p=P, t=4))
-        for h in range(2):
-            nc.sync.dma_start(out=wi[:, 0, 2 * h : 2 * h + 2, :], in_=wi_src[0][:, 2 * h : 2 * h + 2, :])
-        load_w4(1)
-        load_w4s(1)
-        nc.sync.dma_start(out=wi[:, 1], in_=wi_src[1])
-        c_src = codes.rearrange("(r p) k -> p r k", p=P)
-        for h in range(2):
-            nc.sync.dma_start(out=craw[:, 2 * h : 2 * h + 2, :], in_=c_src[:, 2 * h : 2 * h + 2, :])
-        load_w4(2)
-        load_wu(1, 0, 2)
-        load_wu(1, 2, 4)
-        nc.sync.dma_start(out=bcol[:], in_=bias.rearrange("(g p t) -> p g t", p=P, t=4))
-        nc.sync.dma_start(out=gcol[:], in_=gain.rearrange("(g p t) -> p g t", p=P, t=4))
 
         def copy_out(eng, out, in_):
             if eng == "S":
@@ -137,43 +117,45 @@ def tile_prefix_tuning_kv_s11_kernel(
                     )
             return b
 
-        banks = {}
-        wux = {}
-
         def drain_wu(g, t, b, eng):
-            x = wst.tile([P, 2, 128, 4], BF16, name="wux", tag="wux", align_bytes=64)
-            wux[(g, t)] = x
-            copy_out(eng, x[:].bitcast(F32), b[:].rearrange("p (a u r) -> p a r u", a=2, u=2))
+            copy_out(eng, wux[g][t][:].bitcast(F32), b[:].rearrange("p (a u r) -> p a r u", a=2, u=2))
+
+        def turn_wu(g, t, eng):
+            drain_wu(g, t, turn(wu_raw[g][t][:].bitcast(F32)), eng)
 
         def quant_wu(g, t):
-            x = wux[(g, t)]
             nc.vector.quantize_mx(
                 out=wuq[g][:, t, :].bitcast(FP8X4),
                 scales=wus[g][:, t, :],
-                in_=x[:].rearrange("p a r j -> p (a r j)"),
+                in_=wux[g][t][:].rearrange("p a r j -> p (a r j)"),
             )
 
         def drain_c(r, b, eng):
             copy_out(
                 eng,
-                cg[:, :, 128 * r : 128 * r + 128, :].bitcast(F32),
+                cg[r // 2][:, :, 128 * (r % 2) : 128 * (r % 2) + 128, :].bitcast(F32),
                 b[:].rearrange("p (a u r) -> p a r u", a=2, u=2),
             )
 
-        def quant_c(g):
+        def turn_c(r, eng):
+            drain_c(r, turn(craw[r][:].bitcast(F32)), eng)
+
+        def quant_c(s):
             nc.vector.quantize_mx(
-                out=cq[:, g, :].bitcast(FP8X4), scales=cs[:, g, :], in_=cg[:, g].rearrange("p n j -> p (n j)")
+                out=cq[s][:].rearrange("p g n -> p (g n)").bitcast(FP8X4),
+                scales=cs[s][:].rearrange("p g n -> p (g n)"),
+                in_=cg[s][:].rearrange("p g n j -> p (g n j)"),
             )
 
-        def widen(g, t, eng="V"):
-            if eng == "S":
-                nc.scalar.activation(
-                    out=wb[:, g, t, :], in_=wi[:, g, t, :].bitcast(FP8), func=COPY, scale=wisc[:, g, t : t + 1]
-                )
-                return
+        def widen_s(g, t):
+            nc.scalar.activation(
+                out=wb[g][:, t, :], in_=wi[g][:, t, :].bitcast(FP8), func=COPY, scale=wisc[:, g, t : t + 1]
+            )
+
+        def widen(g, t):
             nc.vector.tensor_scalar(
-                out=wb[:, g, t, :],
-                in0=wi[:, g, t, :].bitcast(FP8),
+                out=wb[g][:, t, :],
+                in0=wi[g][:, t, :].bitcast(FP8),
                 scalar1=wisc[:, g, t : t + 1],
                 scalar2=None,
                 op0=MULT,
@@ -182,190 +164,230 @@ def tile_prefix_tuning_kv_s11_kernel(
         def lace(g, h):
             nc.vector.tensor_copy(
                 out=wg[:, g, h, :].rearrange("p (t m j) -> p m j t", t=4, j=4),
-                in_=wb[:, g, :, 512 * h : 512 * h + 512].rearrange("p j (m t) -> p m j t", t=4),
+                in_=wb[g][:, :, 512 * h : 512 * h + 512].rearrange("p j (m t) -> p m j t", t=4),
             )
 
         def quant_wi(g, h):
-            nc.vector.quantize_mx(
-                out=wq[:, g, h, :].bitcast(FP8X4), scales=ws[:, g, h, :], in_=wg[:, g, h, :]
-            )
+            nc.vector.quantize_mx(out=wq[:, g, h, :].bitcast(FP8X4), scales=ws[:, g, h, :], in_=wg[:, g, h, :])
 
-        mx_tiles = {}
-
-        def unit_part(g, c, b, ts):
-            i = min(c // 4, 2)
-            n = 128 * c - cuts[i]
-            j = min(c // 4, 1)
-            m = 128 * c - scuts[j]
+        def unit_part(g, u, b, ts):
+            n = 128 * (u % 4)
+            j = min(u // 4, 1)
+            m = 128 * u - scuts[j]
             for t in ts:
                 for a in range(2):
                     nc.tensor.matmul_mx(
                         out=b[:, 128 * t : 128 * t + 128],
                         lhsT=wuq[g][:, t, 128 * a : 128 * a + 128].bitcast(FP8X4),
                         lhsT_scale=wus[g][:, t, 128 * a : 128 * a + 128],
-                        rhs=w4[i][:, a, 2 * n : 2 * n + 256].bitcast(FP4X4),
+                        rhs=w4[u // 4][:, a, 2 * n : 2 * n + 256].bitcast(FP4X4),
                         rhs_scale=w4s[j][:, a, m : m + 128],
                         start=(a == 0),
                         stop=(a == 1),
                     )
             return b
 
-        def unit(g, c):
-            if g == 0 and c < 4:
-                if c == 0:
-                    for i in range(4):
-                        banks["U00%d" % i] = bank()
-                for i in range(4):
-                    unit_part(0, i, banks["U00%d" % i], [c])
-                return banks["U00%d" % c]
-            return unit_part(g, c, bank(), range(4))
+        def drain_m(g, u, b, eng):
+            copy_out(eng, mx[g][u // 4][:, u % 4], b[:].rearrange("p (t n) -> p n t", t=4))
 
-        def drain_m(g, c, b, eng):
-            if (g, c // 2) not in mx_tiles:
-                x = mst.tile([P, 2, 128, 4], BF16, name="mx", tag="mx", align_bytes=64)
-                mx_tiles[(g, c // 2)] = x
-            x = mx_tiles[(g, c // 2)]
-            copy_out(eng, x[:, c % 2], b[:].rearrange("p (t n) -> p n t", t=4))
-
-        def quant_m(g, d):
-            x = mx_tiles[(g, d)]
+        def quant_m(g, u0, u1):
             nc.vector.quantize_mx(
-                out=mq[g][:, 256 * d : 256 * d + 256].bitcast(FP8X4),
-                scales=ms[g][:, 256 * d : 256 * d + 256],
-                in_=x[:].rearrange("p i n j -> p (i n j)"),
+                out=mq[g][:, 128 * u0 : 128 * u1].bitcast(FP8X4),
+                scales=ms[g][:, 128 * u0 : 128 * u1],
+                in_=mx[g][u0 // 4][:, u0 % 4 : (u1 - 1) % 4 + 1].rearrange("p i n j -> p (i n j)"),
             )
 
-        def hidden(h, t):
+        def hidden(s, h, v):
             b = bank()
-            for g in range(2):
-                nc.tensor.matmul_mx(
-                    out=b[:],
-                    lhsT=wq[:, g, h, 128 * t : 128 * t + 128].bitcast(FP8X4),
-                    lhsT_scale=ws[:, g, h, 128 * t : 128 * t + 128],
-                    rhs=cq[:, g, :].bitcast(FP8X4),
-                    rhs_scale=cs[:, g, :],
-                    start=(g == 0),
-                    stop=(g == 1),
+            for e in range(2):
+                t = 2 * v + e
+                for g in range(2):
+                    nc.tensor.matmul_mx(
+                        out=b[:, HALF * e : HALF * e + HALF],
+                        lhsT=wq[:, g, h, 128 * t : 128 * t + 128].bitcast(FP8X4),
+                        lhsT_scale=ws[:, g, h, 128 * t : 128 * t + 128],
+                        rhs=cq[s][:, g, :].bitcast(FP8X4),
+                        rhs_scale=cs[s][:, g, :],
+                        start=(g == 0),
+                        stop=(g == 1),
+                    )
+            for e in range(2):
+                t = 2 * v + e
+                nc.scalar.activation(
+                    out=th[s][h][:, t, :], in_=b[:, HALF * e : HALF * e + HALF], func=TANH, bias=bcol[:, h, t : t + 1]
                 )
-            return b
 
-        def drain_h(h, t, b):
-            nc.scalar.activation(out=th[h][:, t, :], in_=b[:], func=TANH, bias=bcol[:, h, t : t + 1])
-
-        def gains(h):
+        def gains(s, h):
             nc.vector.tensor_tensor(
-                out=hg[h][:].rearrange("p (c i) t -> p c t i", i=2),
-                in0=th[h][:].rearrange("p t (c i) -> p c t i", i=2),
-                in1=gcol[:, h, :].unsqueeze(1).unsqueeze(3).to_broadcast([P, ROWS // 2, 4, 2]),
+                out=hg[s][:, h].rearrange("p (c i) t -> p c t i", i=2),
+                in0=th[s][h][:].rearrange("p t (c i) -> p c t i", i=2),
+                in1=gcol[:, h, :].unsqueeze(1).unsqueeze(3).to_broadcast([P, HALF // 2, 4, 2]),
                 op=MULT,
             )
 
-        def quant_h(h):
+        def quant_h(s, h):
             nc.vector.quantize_mx(
-                out=hq[h][:].bitcast(FP8X4), scales=hs[h][:], in_=hg[h][:].rearrange("p n j -> p (n j)")
+                out=hq[s][:, h, :].bitcast(FP8X4), scales=hs[s][:, h, :], in_=hg[s][:, h].rearrange("p n j -> p (n j)")
             )
 
-        def final(i, c):
+        def final(i, n0, n1):
             b = bank()
             for g in range(2):
                 nc.tensor.matmul_mx(
-                    out=b[:],
-                    lhsT=hq[g][:, 128 * i : 128 * i + 128].bitcast(FP8X4),
-                    lhsT_scale=hs[g][:, 128 * i : 128 * i + 128],
-                    rhs=mq[g][:, 512 * c : 512 * c + 512].bitcast(FP8X4),
-                    rhs_scale=ms[g][:, 512 * c : 512 * c + 512],
+                    out=b[:, 0 : n1 - n0],
+                    lhsT=hq[i // 2][:, g, 128 * (i % 2) : 128 * (i % 2) + 128].bitcast(FP8X4),
+                    lhsT_scale=hs[i // 2][:, g, 128 * (i % 2) : 128 * (i % 2) + 128],
+                    rhs=mq[g][:, n0:n1].bitcast(FP8X4),
+                    rhs_scale=ms[g][:, n0:n1],
                     start=(g == 0),
                     stop=(g == 1),
                 )
             return b
 
-        def drain_y(i, c, b, eng):
+        def drain_y(i, n0, n1, b, eng):
             y = yst.tile([P, 512], F32, name="y", tag="y", align_bytes=64)
-            dst = (keys if c < 2 else values)[128 * i : 128 * i + 128, 512 * (c % 2) : 512 * (c % 2) + 512]
-            parts = ((0, 512, eng),) if eng in "SV" else ((0, 256, "V"), (256, 512, "S"))
-            for n0, n1, e in parts:
-                copy_out(e, y[:, n0:n1], b[:, n0:n1])
-                nc.sync.dma_start(out=dst[:, n0:n1], in_=y[:, n0:n1])
+            dst = (keys if n0 < 1024 else values)[128 * i : 128 * i + 128, n0 % 1024 : n0 % 1024 + n1 - n0]
+            copy_out(eng, y[:, 0 : n1 - n0], b[:, 0 : n1 - n0])
+            nc.sync.dma_start(out=dst, in_=y[:, 0 : n1 - n0])
 
+        def units(g, u0, u1, engs):
+            for u in range(u0, u1):
+                drain_m(g, u, unit_part(g, u, bank(), range(4)), engs[(u - u0) % len(engs)])
 
-        def units(g, c0, c1, engs):
-            for c in range(c0, c1):
-                drain_m(g, c, unit_part(g, c, bank(), range(4)), engs[c % len(engs)])
+        def hiddens(s, h):
+            for v in range(2):
+                hidden(s, h, v)
 
-        def hiddens(h):
-            for t in range(4):
-                drain_h(h, t, hidden(h, t))
+        def unit(g, u):
+            return unit_part(g, u, bank(), range(4))
 
-        def finals(c, engs):
-            for i in range(4):
-                drain_y(i, c, final(i, c), engs[i])
+        def out_tile(i, n0, n1, eng):
+            drain_y(i, n0, n1, final(i, n0, n1), eng)
+
+        def finals(s, c, engs):
+            for i in range(2):
+                out_tile(2 * s + i, 512 * c, 512 * c + 512, engs[i])
+
+        def dummies(d, n):
+            for i in range(n):
+                nc.tensor.matmul(d[:], lhsT=zeros[:, 0:128], rhs=zeros[:], start=True, stop=True)
+
+        nc.vector.memset(zeros[:], 0.0)
+        for i in range(2):
+            nc.vector.memset(w4s[i][:].rearrange("p a n -> p (a n)").bitcast(I32), 0)
+        nc.vector.memset(warm[:], 0.0)
+        nc.scalar.activation(out=warm[:, 1:2], in_=warm[:, 0:1], func=TANH)
+
+        load_wu(0, 0)
+        load_wu(0, 1)
+        load_w4s(0)
+        load_wu(0, 2)
+        load_wu(0, 3)
+        load_w4(0)
+        nc.sync.dma_start(out=wisc[:], in_=w_in_scale.rearrange("(g p t) o -> p g (t o)", p=P, t=4))
+        load_wi(0, 0, 2)
+        load_wi(0, 2, 4)
+        load_w4(1)
+        load_w4s(1)
+        load_w4(2)
+        load_wi(1, 0, 4)
+        for t in range(4):
+            load_wu(1, t)
+        load_w4(3)
+        for r in range(4):
+            load_c(r)
+        nc.sync.dma_start(out=bcol[:], in_=bias.rearrange("(g p t) -> p g t", p=P, t=4))
+        nc.sync.dma_start(out=gcol[:], in_=gain.rearrange("(g p t) -> p g t", p=P, t=4))
 
         d = bank()
-        for i in range(3):
-            nc.tensor.matmul(d[:], lhsT=zeros[:, 0:128], rhs=zeros[:], start=True, stop=True)
-
+        dummies(d, 3)
+        turned = []
         for t in range(4):
-            drain_wu(0, t, turn(wu_raw[0][:, t, :].bitcast(F32)), "SSVS"[t])
-            if t > 0:
-                quant_wu(0, t - 1)
+            turned.append(turn(wu_raw[0][t][:].bitcast(F32)))
+            if t % 2 == 0:
+                dummies(d, 1)
+        drain_wu(0, 0, turned[0], "S")
+        drain_wu(0, 1, turned[1], "S")
+        quant_wu(0, 0)
+        drain_wu(0, 2, turned[2], "V")
+        quant_wu(0, 1)
+        drain_wu(0, 3, turned[3], "S")
+        quant_wu(0, 2)
         quant_wu(0, 3)
+        widen_s(0, 0)
         first = []
-        for c in range(4):
+        for u in range(4):
             b = bank()
             first.append(b)
         for t in range(4):
-            for c in range(4):
-                unit_part(0, c, first[c], [t])
-        for c in range(4):
-            drain_m(0, c, first[c], "S")
-        for g in range(2):
-            for t in range(4):
-                widen(g, t)
+            for u in range(4):
+                unit_part(0, u, first[u], [t])
+        for u in range(4):
+            drain_m(0, u, first[u], "S")
+        for t in range(1, 4):
+            widen(0, t)
+        lace(0, 0)
         units(0, 4, 8, "S")
-        for r in range(4):
-            drain_c(r, turn(craw[:, r, :].bitcast(F32)), "S")
-        for g in range(2):
-            lace(g, 0)
-        for g in range(2):
-            quant_wi(g, 0)
-        for g in range(2):
-            quant_c(g)
-        units(0, 8, 12, "S")
+        lace(0, 1)
+        held = unit(0, 8)
         for t in range(4):
-            drain_wu(1, t, turn(wu_raw[1][:, t, :].bitcast(F32)), "S")
-        for g in range(2):
-            lace(g, 1)
+            widen(1, t)
+        drain_m(0, 8, held, "V")
+        units(0, 9, 12, "S")
+        quant_wi(0, 0)
+        quant_wi(0, 1)
+        for t in range(4):
+            turn_wu(1, t, "SVSS"[t])
+        lace(1, 0)
+        units(0, 12, 14, "S")
         for t in range(4):
             quant_wu(1, t)
-        for g in range(2):
-            quant_wi(g, 1)
-        units(0, 12, 16, "S")
-        hiddens(0)
-        units(1, 0, 4, "S")
-        hiddens(1)
-        quant_m(0, 0)
-        gains(0)
-        quant_m(0, 1)
-        quant_h(0)
-        quant_m(1, 0)
-        quant_m(1, 1)
-        gains(1)
-        quant_m(0, 2)
-        quant_h(1)
-        units(1, 4, 12, "S")
-        quant_m(0, 3)
-        for d in (2, 3):
-            quant_m(1, d)
-        for g in range(2):
-            for d in (4, 5):
-                quant_m(g, d)
-        finals(0, "SSVS")
-        for d in (6, 7):
-            quant_m(0, d)
-        finals(1, "SVSV")
+        lace(1, 1)
+        for r in range(4):
+            turn_c(r, "S")
+        quant_wi(1, 0)
+        quant_wi(1, 1)
+        units(0, 14, 16, "S")
+        quant_c(0)
+        units(1, 0, 2, "VS")
+        quant_m(0, 0, 4)
+        quant_c(1)
+        units(1, 2, 4, "VS")
+        quant_m(0, 4, 8)
+        hiddens(0, 0)
+        quant_m(1, 0, 4)
+        hiddens(0, 1)
+        gains(0, 0)
+        units(1, 4, 6, "S")
+        gains(0, 1)
+        quant_h(0, 0)
+        units(1, 6, 7, "S")
+        quant_m(0, 8, 12)
+        quant_h(0, 1)
+
+        units(1, 7, 8, "S")
+        hiddens(1, 0)
+        quant_m(1, 4, 8)
+        hiddens(1, 1)
+        gains(1, 0)
+        finals(0, 0, "SS")
+        gains(1, 1)
+        quant_h(1, 0)
+        finals(0, 1, "VS")
+        quant_h(1, 1)
+        units(1, 8, 12, "SVSS")
+        quant_m(0, 12, 16)
+        finals(1, 0, "VS")
+        quant_m(1, 8, 12)
         units(1, 12, 14, "SV")
-        quant_m(1, 6)
-        units(1, 14, 16, "SV")
-        quant_m(1, 7)
-        finals(2, "SVSV")
-        finals(3, "SVS2")
+        finals(1, 1, "SS")
+        quant_m(1, 12, 14)
+        units(1, 14, 16, "VS")
+        out_tile(0, 1024, 1536, "V")
+        quant_m(1, 14, 16)
+        out_tile(1, 1024, 1536, "S")
+        finals(1, 2, "VS")
+        finals(0, 3, "VS")
+        out_tile(2, 1536, 2048, "V")
+        out_tile(3, 1536, 1792, "S")
+        out_tile(3, 1792, 2048, "V")

@@ -27,7 +27,8 @@ def tile_prefix_tuning_kv_s11_kernel(
     nc = tc.nc
     with ExitStack() as ctx:
         keep = ctx.enter_context(tc.tile_pool(name="keep", bufs=1))
-        yst = ctx.enter_context(tc.tile_pool(name="yst", bufs=12))
+        yst = ctx.enter_context(tc.tile_pool(name="yst", bufs=10))
+        sst = ctx.enter_context(tc.tile_pool(name="sst", bufs=4))
         psum = ctx.enter_context(tc.psum_pool(name="psum", bufs=8))
 
         def sb(name, shape, dtype):
@@ -115,6 +116,20 @@ def tile_prefix_tuning_kv_s11_kernel(
                         words[:, 256 * a + u : 256 * (a + 1) : 2],
                         ident[:],
                     )
+            return b
+
+        def split(raw):
+            x = sst.tile([P, 512], F32, name="split", tag="split", align_bytes=64)
+            nc.vector.tensor_copy(
+                out=x[:].rearrange("p (a u c i) -> p a c u i", a=2, u=2, i=4),
+                in_=raw[:].bitcast(F32).rearrange("p (a c i u) -> p a c u i", a=2, u=2, i=4),
+            )
+            return x
+
+        def turn_split(x):
+            b = bank()
+            for i in range(4):
+                nc.tensor.transpose(b[:, 128 * i : 128 * i + 128], x[:, 128 * i : 128 * i + 128], ident[:])
             return b
 
         def drain_wu(g, t, b, eng):
@@ -280,9 +295,9 @@ def tile_prefix_tuning_kv_s11_kernel(
 
         load_wu(0, 0)
         load_wu(0, 1)
-        load_w4s(0)
         load_wu(0, 2)
         load_wu(0, 3)
+        load_w4s(0)
         load_w4(0)
         nc.sync.dma_start(out=wisc[:], in_=w_in_scale.rearrange("(g p t) o -> p g (t o)", p=P, t=4))
         load_wi(0, 0, 2)
@@ -301,20 +316,16 @@ def tile_prefix_tuning_kv_s11_kernel(
 
         d = bank()
         dummies(d, 3)
-        turned = []
         for t in range(4):
-            turned.append(turn(wu_raw[0][t][:].bitcast(F32)))
-            if t % 2 == 0:
+            b = turn_split(split(wu_raw[0][t]))
+            if t < 2:
                 dummies(d, 1)
-        drain_wu(0, 0, turned[0], "S")
-        drain_wu(0, 1, turned[1], "S")
-        quant_wu(0, 0)
-        drain_wu(0, 2, turned[2], "V")
-        quant_wu(0, 1)
-        drain_wu(0, 3, turned[3], "S")
-        quant_wu(0, 2)
+            drain_wu(0, t, b, "S")
+        for t in range(3):
+            quant_wu(0, t)
+        widen(0, 0)
         quant_wu(0, 3)
-        widen_s(0, 0)
+        widen_s(0, 1)
         first = []
         for u in range(4):
             b = bank()
@@ -324,70 +335,77 @@ def tile_prefix_tuning_kv_s11_kernel(
                 unit_part(0, u, first[u], [t])
         for u in range(4):
             drain_m(0, u, first[u], "S")
-        for t in range(1, 4):
+        for t in range(2, 4):
             widen(0, t)
+        parts = []
         lace(0, 0)
         units(0, 4, 8, "S")
         lace(0, 1)
         held = unit(0, 8)
+        units(0, 9, 12, "S")
+        parts = [split(wu_raw[1][t]) for t in range(4)]
+        drain_m(0, 8, held, "V")
+        for t in range(4):
+            drain_wu(1, t, turn_split(parts[t]), "S")
         for t in range(4):
             widen(1, t)
-        drain_m(0, 8, held, "V")
-        units(0, 9, 12, "S")
-        quant_wi(0, 0)
-        quant_wi(0, 1)
-        for t in range(4):
-            turn_wu(1, t, "SVSS"[t])
-        lace(1, 0)
-        units(0, 12, 14, "S")
+        held = unit(0, 12)
+        units(0, 13, 16, "S")
+        parts = [split(craw[r]) for r in range(4)]
         for t in range(4):
             quant_wu(1, t)
-        lace(1, 1)
+        drain_m(0, 12, held, "V")
         for r in range(4):
-            turn_c(r, "S")
+            drain_c(r, turn_split(parts[r]), "S")
+        lace(1, 0)
+        lace(1, 1)
+        units(1, 0, 1, "S")
+        held = unit(1, 1)
+        units(1, 2, 4, "S")
+        quant_wi(0, 0)
+        drain_m(1, 1, held, "V")
         quant_wi(1, 0)
-        quant_wi(1, 1)
-        units(0, 14, 16, "S")
+        held = unit(1, 4)
+        units(1, 5, 8, "S")
         quant_c(0)
-        units(1, 0, 2, "VS")
-        quant_m(0, 0, 4)
-        quant_c(1)
-        units(1, 2, 4, "VS")
-        quant_m(0, 4, 8)
+        quant_wi(0, 1)
+        drain_m(1, 4, held, "V")
+        quant_wi(1, 1)
         hiddens(0, 0)
-        quant_m(1, 0, 4)
+        quant_c(1)
+        quant_m(0, 0, 4)
         hiddens(0, 1)
+        quant_m(1, 0, 4)
         gains(0, 0)
-        units(1, 4, 6, "S")
+        units(1, 8, 12, "S")
         gains(0, 1)
         quant_h(0, 0)
-        units(1, 6, 7, "S")
-        quant_m(0, 8, 12)
+        quant_m(0, 4, 8)
         quant_h(0, 1)
-
-        units(1, 7, 8, "S")
         hiddens(1, 0)
         quant_m(1, 4, 8)
         hiddens(1, 1)
+        quant_m(0, 8, 12)
         gains(1, 0)
         finals(0, 0, "SS")
+        units(1, 12, 13, "S")
+        quant_m(1, 8, 12)
         gains(1, 1)
         quant_h(1, 0)
-        finals(0, 1, "VS")
-        quant_h(1, 1)
-        units(1, 8, 12, "SVSS")
         quant_m(0, 12, 16)
-        finals(1, 0, "VS")
-        quant_m(1, 8, 12)
-        units(1, 12, 14, "SV")
-        finals(1, 1, "SS")
+        quant_h(1, 1)
+        finals(0, 1, "SS")
+        units(1, 13, 14, "S")
+        finals(0, 2, "VS")
+        units(1, 14, 15, "V")
+        finals(1, 0, "SV")
+        out_tile(2, 512, 1024, "S")
         quant_m(1, 12, 14)
-        units(1, 14, 16, "VS")
-        out_tile(0, 1024, 1536, "V")
+        units(1, 15, 16, "V")
+        out_tile(3, 512, 1024, "S")
         quant_m(1, 14, 16)
-        out_tile(1, 1024, 1536, "S")
-        finals(1, 2, "VS")
-        finals(0, 3, "VS")
-        out_tile(2, 1536, 2048, "V")
-        out_tile(3, 1536, 1792, "S")
-        out_tile(3, 1792, 2048, "V")
+        finals(1, 2, "SV")
+        finals(0, 3, "SV")
+        out_tile(2, 1536, 2048, "S")
+        out_tile(3, 1536, 1792, "V")
+        out_tile(3, 1792, 2048, "S")

@@ -323,8 +323,8 @@ def tile_prefix_tuning_kv_s11_kernel(
             drain_wu(0, t, b, "S")
         for t in range(3):
             quant_wu(0, t)
-        widen(0, 0)
         quant_wu(0, 3)
+        widen(0, 0)
         widen_s(0, 1)
         first = []
         for u in range(4):
@@ -349,12 +349,11 @@ def tile_prefix_tuning_kv_s11_kernel(
             drain_wu(1, t, turn_split(parts[t]), "S")
         for t in range(4):
             widen(1, t)
-        held = unit(0, 12)
+        units(0, 12, 13, "S")
         units(0, 13, 16, "S")
         parts = [split(craw[r]) for r in range(4)]
         for t in range(4):
             quant_wu(1, t)
-        drain_m(0, 12, held, "V")
         for r in range(4):
             drain_c(r, turn_split(parts[r]), "S")
         lace(1, 0)
@@ -365,23 +364,23 @@ def tile_prefix_tuning_kv_s11_kernel(
         quant_wi(0, 0)
         drain_m(1, 1, held, "V")
         quant_wi(1, 0)
-        held = unit(1, 4)
+        units(1, 4, 5, "S")
         units(1, 5, 8, "S")
         quant_c(0)
         quant_wi(0, 1)
-        drain_m(1, 4, held, "V")
         quant_wi(1, 1)
+        units(1, 8, 9, "S")
         hiddens(0, 0)
         quant_c(1)
         quant_m(0, 0, 4)
         hiddens(0, 1)
         quant_m(1, 0, 4)
         gains(0, 0)
-        units(1, 8, 12, "S")
+        units(1, 9, 12, "S")
         gains(0, 1)
         quant_h(0, 0)
-        quant_m(0, 4, 8)
         quant_h(0, 1)
+        quant_m(0, 4, 8)
         hiddens(1, 0)
         quant_m(1, 4, 8)
         hiddens(1, 1)
@@ -392,11 +391,11 @@ def tile_prefix_tuning_kv_s11_kernel(
         quant_m(1, 8, 12)
         gains(1, 1)
         quant_h(1, 0)
-        quant_m(0, 12, 16)
         quant_h(1, 1)
+        quant_m(0, 12, 16)
         finals(0, 1, "SS")
         units(1, 13, 14, "S")
-        finals(0, 2, "VS")
+        finals(0, 2, "SS")
         units(1, 14, 15, "V")
         finals(1, 0, "SV")
         out_tile(2, 512, 1024, "S")

@@ -64,7 +64,6 @@ def tile_prefix_tuning_kv_s11_kernel(
         mq = [sb("mq%d" % g, [P, N], U32) for g in range(2)]
         ms = [sb("ms%d" % g, [P, N], U8) for g in range(2)]
         warm = sb("warm", [P, 2], F32)
-        zeros = sb("zeros", [P, 512], BF16)
 
         ctx.enter_context(tc.manual_schedule())
 
@@ -283,11 +282,6 @@ def tile_prefix_tuning_kv_s11_kernel(
             for i in range(2):
                 out_tile(2 * s + i, 512 * c, 512 * c + 512, engs[i])
 
-        def dummies(d, n):
-            for i in range(n):
-                nc.tensor.matmul(d[:], lhsT=zeros[:, 0:128], rhs=zeros[:], start=True, stop=True)
-
-        nc.vector.memset(zeros[:], 0.0)
         for i in range(2):
             nc.vector.memset(w4s[i][:].rearrange("p a n -> p (a n)").bitcast(I32), 0)
         nc.vector.memset(warm[:], 0.0)
@@ -314,12 +308,8 @@ def tile_prefix_tuning_kv_s11_kernel(
         nc.sync.dma_start(out=bcol[:], in_=bias.rearrange("(g p t) -> p g t", p=P, t=4))
         nc.sync.dma_start(out=gcol[:], in_=gain.rearrange("(g p t) -> p g t", p=P, t=4))
 
-        d = bank()
-        dummies(d, 3)
         for t in range(4):
             b = turn_split(split(wu_raw[0][t]))
-            if t < 2:
-                dummies(d, 1)
             drain_wu(0, t, b, "S")
         for t in range(3):
             quant_wu(0, t)

@@ -63,7 +63,6 @@ def tile_prefix_tuning_kv_s11_kernel(
         mx = [[sb("mx%d%d" % (g, c), [P, 4, 128, 4], BF16) for c in range(4)] for g in range(2)]
         mq = [sb("mq%d" % g, [P, N], U32) for g in range(2)]
         ms = [sb("ms%d" % g, [P, N], U8) for g in range(2)]
-        warm = sb("warm", [P, 2], F32)
 
         ctx.enter_context(tc.manual_schedule())
 
@@ -284,8 +283,6 @@ def tile_prefix_tuning_kv_s11_kernel(
 
         for i in range(2):
             nc.vector.memset(w4s[i][:].rearrange("p a n -> p (a n)").bitcast(I32), 0)
-        nc.vector.memset(warm[:], 0.0)
-        nc.scalar.activation(out=warm[:, 1:2], in_=warm[:, 0:1], func=TANH)
 
         load_wu(0, 0)
         load_wu(0, 1)

@@ -165,10 +165,10 @@ def tile_prefix_tuning_kv_s11_kernel(
                 out=wb[g][:, t, :], in_=wi[g][:, t, :].bitcast(FP8), func=COPY, scale=wisc[:, g, t : t + 1]
             )
 
-        def widen(g, t):
+        def widen(g, t, f0=0, f1=F):
             nc.vector.tensor_scalar(
-                out=wb[g][:, t, :],
-                in0=wi[g][:, t, :].bitcast(FP8),
+                out=wb[g][:, t, f0:f1],
+                in0=wi[g][:, t, f0:f1].bitcast(FP8),
                 scalar1=wisc[:, g, t : t + 1],
                 scalar2=None,
                 op0=MULT,
@@ -263,6 +263,35 @@ def tile_prefix_tuning_kv_s11_kernel(
             copy_out(eng, y[:, 0 : n1 - n0], b[:, 0 : n1 - n0])
             nc.sync.dma_start(out=dst, in_=y[:, 0 : n1 - n0])
 
+        def out_twin(i, n0, engs="VS"):
+            y = yst.tile([P, 512], F32, name="y", tag="y", align_bytes=64)
+            for e in range(2):
+                b = final(i, n0 + 256 * e, n0 + 256 * e + 256)
+                copy_out(engs[e], y[:, 256 * e : 256 * e + 256], b[:, 0:256])
+            dst = (keys if n0 < 1024 else values)[128 * i : 128 * i + 128, n0 % 1024 : n0 % 1024 + 512]
+            nc.sync.dma_start(out=dst, in_=y[:])
+
+        def wide_units(g, c, engs):
+            for t in range(4):
+                b = bank()
+                for a in range(2):
+                    nc.tensor.matmul_mx(
+                        out=b[:],
+                        lhsT=wuq[g][:, t, 128 * a : 128 * a + 128].bitcast(FP8X4),
+                        lhsT_scale=wus[g][:, t, 128 * a : 128 * a + 128],
+                        rhs=w4[c][:, a, :].bitcast(FP4X4),
+                        rhs_scale=w4s[1][:, a, 512 * c - scuts[1] : 512 * c + 512 - scuts[1]],
+                        start=(a == 0),
+                        stop=(a == 1),
+                    )
+                copy_out(engs[t], wb[0][:, t, 512 * (c - 2) : 512 * (c - 1)], b[:])
+
+        def lace_m(g, c):
+            nc.vector.tensor_copy(
+                out=mx[g][c][:].rearrange("p u (x i) t -> p (u x) t i", i=4),
+                in_=wb[0][:, :, 512 * (c - 2) : 512 * (c - 1)].rearrange("p t (x i) -> p x t i", i=4),
+            )
+
         def units(g, u0, u1, engs):
             for u in range(u0, u1):
                 drain_m(g, u, unit_part(g, u, bank(), range(4)), engs[(u - u0) % len(engs)])
@@ -322,8 +351,9 @@ def tile_prefix_tuning_kv_s11_kernel(
                 unit_part(0, u, first[u], [t])
         for u in range(4):
             drain_m(0, u, first[u], "S")
-        for t in range(2, 4):
-            widen(0, t)
+        widen(0, 2)
+        widen(0, 3, 0, 512)
+        widen(0, 3, 512, F)
         parts = []
         lace(0, 0)
         units(0, 4, 8, "S")
@@ -336,8 +366,7 @@ def tile_prefix_tuning_kv_s11_kernel(
             drain_wu(1, t, turn_split(parts[t]), "S")
         for t in range(4):
             widen(1, t)
-        units(0, 12, 13, "S")
-        units(0, 13, 16, "S")
+        wide_units(0, 3, "SSSS")
         parts = [split(craw[r]) for r in range(4)]
         for t in range(4):
             quant_wu(1, t)
@@ -379,19 +408,19 @@ def tile_prefix_tuning_kv_s11_kernel(
         gains(1, 1)
         quant_h(1, 0)
         quant_h(1, 1)
-        quant_m(0, 12, 16)
+        lace_m(0, 3)
         finals(0, 1, "SS")
         units(1, 13, 14, "S")
         finals(0, 2, "SS")
-        units(1, 14, 15, "V")
+        units(1, 14, 15, "S")
+        quant_m(1, 12, 14)
+        quant_m(0, 12, 16)
         finals(1, 0, "SV")
         out_tile(2, 512, 1024, "S")
-        quant_m(1, 12, 14)
         units(1, 15, 16, "V")
-        out_tile(3, 512, 1024, "S")
+        out_twin(3, 512, "SS")
         quant_m(1, 14, 16)
-        finals(1, 2, "SV")
-        finals(0, 3, "SV")
-        out_tile(2, 1536, 2048, "S")
-        out_tile(3, 1536, 1792, "V")
-        out_tile(3, 1792, 2048, "S")
+        out_twin(2, 1024)
+        out_twin(3, 1024)
+        for i in range(4):
+            out_twin(i, 1536)

@@ -50,7 +50,8 @@ def tile_prefix_tuning_kv_s11_kernel(
         cs = [sb("cs%d" % s, [P, 2, HALF], U8) for s in range(2)]
         wi = [sb("wi%d" % g, [P, 4, F], U8) for g in range(2)]
         wisc = sb("wisc", [P, 2, 4], F32)
-        wb = [sb("wb%d" % g, [P, 4, F], BF16) for g in range(2)]
+        wb0 = [sb("wb0%d" % h, [P, 4, 512], BF16) for h in range(2)]
+        wb1 = sb("wb1", [P, 4, F], BF16)
         wg = sb("wg", [P, 2, 2, 2048], BF16)
         wq = sb("wq", [P, 2, 2, 512], U32)
         ws = sb("ws", [P, 2, 2, 512], U8)
@@ -104,18 +105,6 @@ def tile_prefix_tuning_kv_s11_kernel(
             b = psum.tile([P, 512], F32, name="bank", tag="bank")
             return b
 
-        def turn(words):
-            b = bank()
-            for a in range(2):
-                for u in range(2):
-                    i = 2 * a + u
-                    nc.tensor.transpose(
-                        b[:, 128 * i : 128 * i + 128],
-                        words[:, 256 * a + u : 256 * (a + 1) : 2],
-                        ident[:],
-                    )
-            return b
-
         def split(raw):
             x = sst.tile([P, 512], F32, name="split", tag="split", align_bytes=64)
             nc.vector.tensor_copy(
@@ -133,9 +122,6 @@ def tile_prefix_tuning_kv_s11_kernel(
         def drain_wu(g, t, b, eng):
             copy_out(eng, wux[g][t][:].bitcast(F32), b[:].rearrange("p (a u r) -> p a r u", a=2, u=2))
 
-        def turn_wu(g, t, eng):
-            drain_wu(g, t, turn(wu_raw[g][t][:].bitcast(F32)), eng)
-
         def quant_wu(g, t):
             nc.vector.quantize_mx(
                 out=wuq[g][:, t, :].bitcast(FP8X4),
@@ -150,9 +136,6 @@ def tile_prefix_tuning_kv_s11_kernel(
                 b[:].rearrange("p (a u r) -> p a r u", a=2, u=2),
             )
 
-        def turn_c(r, eng):
-            drain_c(r, turn(craw[r][:].bitcast(F32)), eng)
-
         def quant_c(s):
             nc.vector.quantize_mx(
                 out=cq[s][:].rearrange("p g n -> p (g n)").bitcast(FP8X4),
@@ -160,24 +143,21 @@ def tile_prefix_tuning_kv_s11_kernel(
                 in_=cg[s][:].rearrange("p g n j -> p (g n j)"),
             )
 
-        def widen_s(g, t):
-            nc.scalar.activation(
-                out=wb[g][:, t, :], in_=wi[g][:, t, :].bitcast(FP8), func=COPY, scale=wisc[:, g, t : t + 1]
-            )
+        def widen(out, g, t, f0, f1, eng):
+            in_ = wi[g][:, t, f0:f1].bitcast(FP8)
+            if eng == "S":
+                nc.scalar.activation(out=out, in_=in_, func=COPY, scale=wisc[:, g, t : t + 1])
+            else:
+                nc.vector.tensor_scalar(out=out, in0=in_, scalar1=wisc[:, g, t : t + 1], scalar2=None, op0=MULT)
 
-        def widen(g, t, f0=0, f1=F):
-            nc.vector.tensor_scalar(
-                out=wb[g][:, t, f0:f1],
-                in0=wi[g][:, t, f0:f1].bitcast(FP8),
-                scalar1=wisc[:, g, t : t + 1],
-                scalar2=None,
-                op0=MULT,
-            )
+        def widen_half(t, h, eng):
+            widen(wb0[h][:, t, :], 0, t, 512 * h, 512 * h + 512, eng)
 
         def lace(g, h):
+            rows = wb0[h][:] if g == 0 else wb1[:, :, 512 * h : 512 * h + 512]
             nc.vector.tensor_copy(
                 out=wg[:, g, h, :].rearrange("p (t m j) -> p m j t", t=4, j=4),
-                in_=wb[g][:, :, 512 * h : 512 * h + 512].rearrange("p j (m t) -> p m j t", t=4),
+                in_=rows.rearrange("p j (m t) -> p m j t", t=4),
             )
 
         def quant_wi(g, h):
@@ -284,12 +264,12 @@ def tile_prefix_tuning_kv_s11_kernel(
                         start=(a == 0),
                         stop=(a == 1),
                     )
-                copy_out(engs[t], wb[0][:, t, 512 * (c - 2) : 512 * (c - 1)], b[:])
+                copy_out(engs[t], wb0[1][:, t, :], b[:])
 
         def lace_m(g, c):
             nc.vector.tensor_copy(
                 out=mx[g][c][:].rearrange("p u (x i) t -> p (u x) t i", i=4),
-                in_=wb[0][:, :, 512 * (c - 2) : 512 * (c - 1)].rearrange("p t (x i) -> p x t i", i=4),
+                in_=wb0[1][:].rearrange("p t (x i) -> p x t i", i=4),
             )
 
         def units(g, u0, u1, engs):
@@ -325,9 +305,9 @@ def tile_prefix_tuning_kv_s11_kernel(
         load_w4(1)
         load_w4s(1)
         load_w4(2)
-        load_wi(1, 0, 4)
         for t in range(4):
             load_wu(1, t)
+        load_wi(1, 0, 4)
         load_w4(3)
         for r in range(4):
             load_c(r)
@@ -340,8 +320,12 @@ def tile_prefix_tuning_kv_s11_kernel(
         for t in range(3):
             quant_wu(0, t)
         quant_wu(0, 3)
-        widen(0, 0)
-        widen_s(0, 1)
+        for t in (0, 2, 3):
+            widen_half(t, 0, "V")
+        widen_half(0, 1, "V")
+        widen_half(1, 0, "S")
+        for t in (1, 2, 3):
+            widen_half(t, 1, "S")
         first = []
         for u in range(4):
             b = bank()
@@ -351,10 +335,6 @@ def tile_prefix_tuning_kv_s11_kernel(
                 unit_part(0, u, first[u], [t])
         for u in range(4):
             drain_m(0, u, first[u], "S")
-        widen(0, 2)
-        widen(0, 3, 0, 512)
-        widen(0, 3, 512, F)
-        parts = []
         lace(0, 0)
         units(0, 4, 8, "S")
         lace(0, 1)
@@ -365,7 +345,7 @@ def tile_prefix_tuning_kv_s11_kernel(
         for t in range(4):
             drain_wu(1, t, turn_split(parts[t]), "S")
         for t in range(4):
-            widen(1, t)
+            widen(wb1[:, t, :], 1, t, 0, F, "V")
         wide_units(0, 3, "SSSS")
         parts = [split(craw[r]) for r in range(4)]
         for t in range(4):
@@ -374,23 +354,20 @@ def tile_prefix_tuning_kv_s11_kernel(
             drain_c(r, turn_split(parts[r]), "S")
         lace(1, 0)
         lace(1, 1)
-        units(1, 0, 1, "S")
-        held = unit(1, 1)
-        units(1, 2, 4, "S")
+        units(1, 0, 7, "S")
+        held = [unit(1, u) for u in (7, 8)]
         quant_wi(0, 0)
-        drain_m(1, 1, held, "V")
         quant_wi(1, 0)
-        units(1, 4, 5, "S")
-        units(1, 5, 8, "S")
         quant_c(0)
         quant_wi(0, 1)
         quant_wi(1, 1)
-        units(1, 8, 9, "S")
         hiddens(0, 0)
         quant_c(1)
         quant_m(0, 0, 4)
         hiddens(0, 1)
         quant_m(1, 0, 4)
+        for u in (7, 8):
+            drain_m(1, u, held[u - 7], "V")
         gains(0, 0)
         units(1, 9, 12, "S")
         gains(0, 1)

@@ -34,6 +34,8 @@ def tile_prefix_tuning_kv_s11_kernel(
         def sb(name, shape, dtype):
             return keep.tile(shape, dtype, name=name, align_bytes=64)
 
+        zeros = sb("zeros", [P, 512], BF16)
+        nc.gpsimd.memset(zeros[:].bitcast(I32), 0)
         ident = sb("ident", [P, P], F32)
         make_identity(nc, ident[:])
 
@@ -42,7 +44,7 @@ def tile_prefix_tuning_kv_s11_kernel(
         wuq = [sb("wuq%d" % g, [P, 4, 256], U32) for g in range(2)]
         wus = [sb("wus%d" % g, [P, 4, 256], U8) for g in range(2)]
         w4 = [sb("w4_%d" % c, [P, 2, 1024], U8) for c in range(4)]
-        scuts = (0, 512, N)
+        scuts = (0, 1024, N)
         w4s = [sb("w4s_%d" % i, [P, 2, scuts[i + 1] - scuts[i]], U8) for i in range(2)]
         craw = [sb("craw%d" % r, [P, K], BF16) for r in range(4)]
         cg = [sb("cg%d" % s, [P, 2, HALF, 4], BF16) for s in range(2)]
@@ -165,7 +167,7 @@ def tile_prefix_tuning_kv_s11_kernel(
 
         def unit_part(g, u, b, ts):
             n = 128 * (u % 4)
-            j = min(u // 4, 1)
+            j = u // 8
             m = 128 * u - scuts[j]
             for t in ts:
                 for a in range(2):
@@ -290,6 +292,11 @@ def tile_prefix_tuning_kv_s11_kernel(
             for i in range(2):
                 out_tile(2 * s + i, 512 * c, 512 * c + 512, engs[i])
 
+        def warm(n):
+            b = bank()
+            for i in range(n):
+                nc.tensor.matmul(out=b[:], lhsT=zeros[:, 0:128], rhs=zeros[:], start=True, stop=True)
+
         for i in range(2):
             nc.vector.memset(w4s[i][:].rearrange("p a n -> p (a n)").bitcast(I32), 0)
 
@@ -314,12 +321,16 @@ def tile_prefix_tuning_kv_s11_kernel(
         nc.sync.dma_start(out=bcol[:], in_=bias.rearrange("(g p t) -> p g t", p=P, t=4))
         nc.sync.dma_start(out=gcol[:], in_=gain.rearrange("(g p t) -> p g t", p=P, t=4))
 
-        for t in range(4):
-            b = turn_split(split(wu_raw[0][t]))
-            drain_wu(0, t, b, "S")
-        for t in range(3):
+        warm(4)
+        drain_wu(0, 0, turn_split(split(wu_raw[0][0])), "S")
+        warm(2)
+        second = turn_split(split(wu_raw[0][1]))
+        for t in (2, 3):
+            drain_wu(0, t, turn_split(split(wu_raw[0][t])), "S")
+        quant_wu(0, 0)
+        drain_wu(0, 1, second, "V")
+        for t in (1, 2, 3):
             quant_wu(0, t)
-        quant_wu(0, 3)
         for t in (0, 2, 3):
             widen_half(t, 0, "V")
         widen_half(0, 1, "V")

@@ -121,6 +121,16 @@ def tile_prefix_tuning_kv_s11_kernel(
                 nc.tensor.transpose(b[:, 128 * i : 128 * i + 128], x[:, 128 * i : 128 * i + 128], ident[:])
             return b
 
+        def turn_half(x, a):
+            b = bank()
+            for u in range(2):
+                i = 2 * a + u
+                nc.tensor.transpose(b[:, 128 * u : 128 * u + 128], x[:, 128 * i : 128 * i + 128], ident[:])
+            return b
+
+        def drain_half(t, a, b, eng):
+            copy_out(eng, wux[0][t][:, a].bitcast(F32), b[:, 0:256].rearrange("p (u r) -> p r u", u=2))
+
         def drain_wu(g, t, b, eng):
             copy_out(eng, wux[g][t][:].bitcast(F32), b[:].rearrange("p (a u r) -> p a r u", a=2, u=2))
 
@@ -324,12 +334,18 @@ def tile_prefix_tuning_kv_s11_kernel(
         warm(4)
         drain_wu(0, 0, turn_split(split(wu_raw[0][0])), "S")
         warm(2)
-        second = turn_split(split(wu_raw[0][1]))
-        for t in (2, 3):
-            drain_wu(0, t, turn_split(split(wu_raw[0][t])), "S")
+        words = split(wu_raw[0][1])
+        drain_half(1, 0, turn_half(words, 0), "S")
+        second = turn_half(words, 1)
+        drain_wu(0, 2, turn_split(split(wu_raw[0][2])), "S")
+        words = split(wu_raw[0][3])
+        fourth = turn_half(words, 0)
+        drain_half(3, 1, turn_half(words, 1), "S")
         quant_wu(0, 0)
-        drain_wu(0, 1, second, "V")
-        for t in (1, 2, 3):
+        drain_half(1, 1, second, "V")
+        quant_wu(0, 1)
+        drain_half(3, 0, fourth, "V")
+        for t in (2, 3):
             quant_wu(0, t)
         for t in (0, 2, 3):
             widen_half(t, 0, "V")

@@ -36,34 +36,37 @@ def tile_prefix_tuning_kv_s11_kernel(
 
         zeros = sb("zeros", [P, 512], BF16)
         nc.gpsimd.memset(zeros[:].bitcast(I32), 0)
+        ident_bf = sb("ident_bf", [P, P], BF16)
+        make_identity(nc, ident_bf[:])
         ident = sb("ident", [P, P], F32)
-        make_identity(nc, ident[:])
 
         wu_raw = [[sb("wu_raw%d%d" % (g, t), [P, D], BF16) for t in range(4)] for g in range(2)]
         wux = [[sb("wux%d%d" % (g, t), [P, 2, 128, 4], BF16) for t in range(4)] for g in range(2)]
-        wuq = [sb("wuq%d" % g, [P, 4, 256], U32) for g in range(2)]
-        wus = [sb("wus%d" % g, [P, 4, 256], U8) for g in range(2)]
-        w4 = [sb("w4_%d" % c, [P, 2, 1024], U8) for c in range(4)]
+        wuq = [[sb("wuq%d%d" % (g, t), [P, 256], U32) for t in range(4)] for g in range(2)]
+        wus = [[sb("wus%d%d" % (g, t), [P, 256], U8) for t in range(4)] for g in range(2)]
+        w4_rest = [sb("w4_%d" % c, [P, 2, 1024], U8) for c in range(4)]
+        w4 = [[x[:, a, :] for a in range(2)] for x in w4_rest]
         scuts = (0, 1024, N)
         w4s = [sb("w4s_%d" % i, [P, 2, scuts[i + 1] - scuts[i]], U8) for i in range(2)]
         craw = [sb("craw%d" % r, [P, K], BF16) for r in range(4)]
         cg = [sb("cg%d" % s, [P, 2, HALF, 4], BF16) for s in range(2)]
         cq = [sb("cq%d" % s, [P, 2, HALF], U32) for s in range(2)]
         cs = [sb("cs%d" % s, [P, 2, HALF], U8) for s in range(2)]
-        wi = [sb("wi%d" % g, [P, 4, F], U8) for g in range(2)]
+        wi_late = sb("wi_late", [P, 4, F], U8)
+        wi = [[sb("wi0%d" % v, [P, 2, F], U8) for v in range(2)], [wi_late[:, 2 * v : 2 * v + 2, :] for v in range(2)]]
         wisc = sb("wisc", [P, 2, 4], F32)
         wb0 = [sb("wb0%d" % h, [P, 4, 512], BF16) for h in range(2)]
         wb1 = sb("wb1", [P, 4, F], BF16)
-        wg = sb("wg", [P, 2, 2, 2048], BF16)
-        wq = sb("wq", [P, 2, 2, 512], U32)
-        ws = sb("ws", [P, 2, 2, 512], U8)
+        wg = [[sb("wg%d%d" % (g, h), [P, 2048], BF16) for h in range(2)] for g in range(2)]
+        wq = [[sb("wq%d%d" % (g, h), [P, 512], U32) for h in range(2)] for g in range(2)]
+        ws = [[sb("ws%d%d" % (g, h), [P, 512], U8) for h in range(2)] for g in range(2)]
         bcol = sb("bcol", [P, 2, 4], BF16)
         gcol = sb("gcol", [P, 2, 4], BF16)
         th = [[sb("th%d%d" % (s, g), [P, 4, HALF], F32) for g in range(2)] for s in range(2)]
-        hg = [sb("hg%d" % s, [P, 2, HALF, 4], BF16) for s in range(2)]
-        hq = [sb("hq%d" % s, [P, 2, HALF], U32) for s in range(2)]
-        hs = [sb("hs%d" % s, [P, 2, HALF], U8) for s in range(2)]
-        mx = [[sb("mx%d%d" % (g, c), [P, 4, 128, 4], BF16) for c in range(4)] for g in range(2)]
+        hg = [[sb("hg%d%d" % (s, h), [P, HALF, 4], BF16) for h in range(2)] for s in range(2)]
+        hq = [[sb("hq%d%d" % (s, h), [P, HALF], U32) for h in range(2)] for s in range(2)]
+        hs = [[sb("hs%d%d" % (s, h), [P, HALF], U8) for h in range(2)] for s in range(2)]
+        mx = [[sb("mx%d%d" % (g, c), [P, 2048], BF16) for c in range(4)] for g in range(2)]
         mq = [sb("mq%d" % g, [P, N], U32) for g in range(2)]
         ms = [sb("ms%d" % g, [P, N], U8) for g in range(2)]
 
@@ -72,6 +75,7 @@ def tile_prefix_tuning_kv_s11_kernel(
         wu_src = w_up.rearrange("(g p t) d -> g t p d", p=P, t=4)
         wi_src = w_in_bytes.rearrange("(g p t) f -> g p t f", p=P, t=4)
         c_src = codes.rearrange("(r p) k -> r p k", p=P)
+        outs = [o.rearrange("(s e p) n -> s e p n", p=P, e=2) for o in (keys, values)]
 
         def load_wu(g, t):
             nc.sync.dma_start(out=wu_raw[g][t][:], in_=wu_src[g][t])
@@ -80,12 +84,17 @@ def tile_prefix_tuning_kv_s11_kernel(
             nc.sync.dma_start(out=craw[r][:], in_=c_src[r])
 
         def load_wi(g, t0, t1):
-            nc.sync.dma_start(out=wi[g][:, t0:t1, :], in_=wi_src[g][:, t0:t1, :])
+            nc.sync.dma_start(out=wi[g][t0 // 2][:], in_=wi_src[g][:, t0:t1, :])
 
         def load_w4(c):
             nc.sync.dma_start(
-                out=w4[c][:].bitcast(I32),
+                out=w4_rest[c][:].bitcast(I32),
                 in_=wkv_words.rearrange("g p b -> p g b")[:, :, 1024 * c : 1024 * c + 1024].bitcast(I32),
+            )
+
+        def load_w4_pass(c, a):
+            nc.sync.dma_start(
+                out=w4[c][a][:].bitcast(I32), in_=wkv_words[a][:, 1024 * c : 1024 * c + 1024].bitcast(I32)
             )
 
         def load_w4s(i):
@@ -107,8 +116,8 @@ def tile_prefix_tuning_kv_s11_kernel(
             b = psum.tile([P, 512], F32, name="bank", tag="bank")
             return b
 
-        def split(raw):
-            x = sst.tile([P, 512], F32, name="split", tag="split", align_bytes=64)
+        def split(raw, spare=None):
+            x = sst.tile([P, 512], F32, name="split", tag="split", align_bytes=64) if spare is None else spare[:].bitcast(F32)
             nc.vector.tensor_copy(
                 out=x[:].rearrange("p (a u c i) -> p a c u i", a=2, u=2, i=4),
                 in_=raw[:].bitcast(F32).rearrange("p (a c i u) -> p a c u i", a=2, u=2, i=4),
@@ -120,6 +129,21 @@ def tile_prefix_tuning_kv_s11_kernel(
             for i in range(4):
                 nc.tensor.transpose(b[:, 128 * i : 128 * i + 128], x[:, 128 * i : 128 * i + 128], ident[:])
             return b
+
+        def turn_plain(t, a):
+            b = bank()
+            for j in range(4):
+                nc.tensor.matmul(
+                    out=b[:, 128 * j : 128 * j + 128],
+                    lhsT=wu_raw[0][t][:, 512 * a + j : 512 * a + 512 : 4],
+                    rhs=ident_bf[:],
+                    start=True,
+                    stop=True,
+                )
+            return b
+
+        def drain_plain(t, a, b, eng):
+            copy_out(eng, wux[0][t][:, a], b[:].rearrange("p (j r) -> p r j", j=4))
 
         def turn_half(x, a):
             b = bank()
@@ -136,8 +160,8 @@ def tile_prefix_tuning_kv_s11_kernel(
 
         def quant_wu(g, t):
             nc.vector.quantize_mx(
-                out=wuq[g][:, t, :].bitcast(FP8X4),
-                scales=wus[g][:, t, :],
+                out=wuq[g][t][:].bitcast(FP8X4),
+                scales=wus[g][t][:],
                 in_=wux[g][t][:].rearrange("p a r j -> p (a r j)"),
             )
 
@@ -156,7 +180,7 @@ def tile_prefix_tuning_kv_s11_kernel(
             )
 
         def widen(out, g, t, f0, f1, eng):
-            in_ = wi[g][:, t, f0:f1].bitcast(FP8)
+            in_ = wi[g][t // 2][:, t % 2, f0:f1].bitcast(FP8)
             if eng == "S":
                 nc.scalar.activation(out=out, in_=in_, func=COPY, scale=wisc[:, g, t : t + 1])
             else:
@@ -165,15 +189,18 @@ def tile_prefix_tuning_kv_s11_kernel(
         def widen_half(t, h, eng):
             widen(wb0[h][:, t, :], 0, t, 512 * h, 512 * h + 512, eng)
 
+        def widen_late(t, h, eng="V"):
+            widen(wb1[:, t, 512 * h : 512 * h + 512], 1, t, 512 * h, 512 * h + 512, eng)
+
         def lace(g, h):
             rows = wb0[h][:] if g == 0 else wb1[:, :, 512 * h : 512 * h + 512]
             nc.vector.tensor_copy(
-                out=wg[:, g, h, :].rearrange("p (t m j) -> p m j t", t=4, j=4),
+                out=wg[g][h][:].rearrange("p (t m j) -> p m j t", t=4, j=4),
                 in_=rows.rearrange("p j (m t) -> p m j t", t=4),
             )
 
         def quant_wi(g, h):
-            nc.vector.quantize_mx(out=wq[:, g, h, :].bitcast(FP8X4), scales=ws[:, g, h, :], in_=wg[:, g, h, :])
+            nc.vector.quantize_mx(out=wq[g][h][:].bitcast(FP8X4), scales=ws[g][h][:], in_=wg[g][h][:])
 
         def unit_part(g, u, b, ts):
             n = 128 * (u % 4)
@@ -183,23 +210,37 @@ def tile_prefix_tuning_kv_s11_kernel(
                 for a in range(2):
                     nc.tensor.matmul_mx(
                         out=b[:, 128 * t : 128 * t + 128],
-                        lhsT=wuq[g][:, t, 128 * a : 128 * a + 128].bitcast(FP8X4),
-                        lhsT_scale=wus[g][:, t, 128 * a : 128 * a + 128],
-                        rhs=w4[u // 4][:, a, 2 * n : 2 * n + 256].bitcast(FP4X4),
+                        lhsT=wuq[g][t][:, 128 * a : 128 * a + 128].bitcast(FP8X4),
+                        lhsT_scale=wus[g][t][:, 128 * a : 128 * a + 128],
+                        rhs=w4[u // 4][a][:, 2 * n : 2 * n + 256].bitcast(FP4X4),
                         rhs_scale=w4s[j][:, a, m : m + 128],
                         start=(a == 0),
                         stop=(a == 1),
                     )
             return b
 
+        def one_pass(g, u, b, t, a):
+            n = 128 * (u % 4)
+            j = u // 8
+            m = 128 * u - scuts[j]
+            nc.tensor.matmul_mx(
+                out=b[:, 128 * t : 128 * t + 128],
+                lhsT=wuq[g][t][:, 128 * a : 128 * a + 128].bitcast(FP8X4),
+                lhsT_scale=wus[g][t][:, 128 * a : 128 * a + 128],
+                rhs=w4[u // 4][a][:, 2 * n : 2 * n + 256].bitcast(FP4X4),
+                rhs_scale=w4s[j][:, a, m : m + 128],
+                start=(a == 0),
+                stop=(a == 1),
+            )
+
         def drain_m(g, u, b, eng):
-            copy_out(eng, mx[g][u // 4][:, u % 4], b[:].rearrange("p (t n) -> p n t", t=4))
+            copy_out(eng, mx[g][u // 4][:, 512 * (u % 4) : 512 * (u % 4) + 512].rearrange("p (n t) -> p n t", t=4), b[:].rearrange("p (t n) -> p n t", t=4))
 
         def quant_m(g, u0, u1):
             nc.vector.quantize_mx(
                 out=mq[g][:, 128 * u0 : 128 * u1].bitcast(FP8X4),
                 scales=ms[g][:, 128 * u0 : 128 * u1],
-                in_=mx[g][u0 // 4][:, u0 % 4 : (u1 - 1) % 4 + 1].rearrange("p i n j -> p (i n j)"),
+                in_=mx[g][u0 // 4][:, 512 * (u0 % 4) : 512 * ((u1 - 1) % 4 + 1)],
             )
 
         def hidden(s, h, v):
@@ -209,8 +250,8 @@ def tile_prefix_tuning_kv_s11_kernel(
                 for g in range(2):
                     nc.tensor.matmul_mx(
                         out=b[:, HALF * e : HALF * e + HALF],
-                        lhsT=wq[:, g, h, 128 * t : 128 * t + 128].bitcast(FP8X4),
-                        lhsT_scale=ws[:, g, h, 128 * t : 128 * t + 128],
+                        lhsT=wq[g][h][:, 128 * t : 128 * t + 128].bitcast(FP8X4),
+                        lhsT_scale=ws[g][h][:, 128 * t : 128 * t + 128],
                         rhs=cq[s][:, g, :].bitcast(FP8X4),
                         rhs_scale=cs[s][:, g, :],
                         start=(g == 0),
@@ -224,7 +265,7 @@ def tile_prefix_tuning_kv_s11_kernel(
 
         def gains(s, h):
             nc.vector.tensor_tensor(
-                out=hg[s][:, h].rearrange("p (c i) t -> p c t i", i=2),
+                out=hg[s][h][:].rearrange("p (c i) t -> p c t i", i=2),
                 in0=th[s][h][:].rearrange("p t (c i) -> p c t i", i=2),
                 in1=gcol[:, h, :].unsqueeze(1).unsqueeze(3).to_broadcast([P, HALF // 2, 4, 2]),
                 op=MULT,
@@ -232,7 +273,7 @@ def tile_prefix_tuning_kv_s11_kernel(
 
         def quant_h(s, h):
             nc.vector.quantize_mx(
-                out=hq[s][:, h, :].bitcast(FP8X4), scales=hs[s][:, h, :], in_=hg[s][:, h].rearrange("p n j -> p (n j)")
+                out=hq[s][h][:].bitcast(FP8X4), scales=hs[s][h][:], in_=hg[s][h][:].rearrange("p n j -> p (n j)")
             )
 
         def final(i, n0, n1):
@@ -240,8 +281,8 @@ def tile_prefix_tuning_kv_s11_kernel(
             for g in range(2):
                 nc.tensor.matmul_mx(
                     out=b[:, 0 : n1 - n0],
-                    lhsT=hq[i // 2][:, g, 128 * (i % 2) : 128 * (i % 2) + 128].bitcast(FP8X4),
-                    lhsT_scale=hs[i // 2][:, g, 128 * (i % 2) : 128 * (i % 2) + 128],
+                    lhsT=hq[i // 2][g][:, 128 * (i % 2) : 128 * (i % 2) + 128].bitcast(FP8X4),
+                    lhsT_scale=hs[i // 2][g][:, 128 * (i % 2) : 128 * (i % 2) + 128],
                     rhs=mq[g][:, n0:n1].bitcast(FP8X4),
                     rhs_scale=ms[g][:, n0:n1],
                     start=(g == 0),
@@ -251,7 +292,7 @@ def tile_prefix_tuning_kv_s11_kernel(
 
         def drain_y(i, n0, n1, b, eng):
             y = yst.tile([P, 512], F32, name="y", tag="y", align_bytes=64)
-            dst = (keys if n0 < 1024 else values)[128 * i : 128 * i + 128, n0 % 1024 : n0 % 1024 + n1 - n0]
+            dst = outs[n0 // 1024][i // 2][i % 2][:, n0 % 1024 : n0 % 1024 + n1 - n0]
             copy_out(eng, y[:, 0 : n1 - n0], b[:, 0 : n1 - n0])
             nc.sync.dma_start(out=dst, in_=y[:, 0 : n1 - n0])
 
@@ -260,7 +301,7 @@ def tile_prefix_tuning_kv_s11_kernel(
             for e in range(2):
                 b = final(i, n0 + 256 * e, n0 + 256 * e + 256)
                 copy_out(engs[e], y[:, 256 * e : 256 * e + 256], b[:, 0:256])
-            dst = (keys if n0 < 1024 else values)[128 * i : 128 * i + 128, n0 % 1024 : n0 % 1024 + 512]
+            dst = outs[n0 // 1024][i // 2][i % 2][:, n0 % 1024 : n0 % 1024 + 512]
             nc.sync.dma_start(out=dst, in_=y[:])
 
         def wide_units(g, c, engs):
@@ -269,9 +310,9 @@ def tile_prefix_tuning_kv_s11_kernel(
                 for a in range(2):
                     nc.tensor.matmul_mx(
                         out=b[:],
-                        lhsT=wuq[g][:, t, 128 * a : 128 * a + 128].bitcast(FP8X4),
-                        lhsT_scale=wus[g][:, t, 128 * a : 128 * a + 128],
-                        rhs=w4[c][:, a, :].bitcast(FP4X4),
+                        lhsT=wuq[g][t][:, 128 * a : 128 * a + 128].bitcast(FP8X4),
+                        lhsT_scale=wus[g][t][:, 128 * a : 128 * a + 128],
+                        rhs=w4[c][a][:].bitcast(FP4X4),
                         rhs_scale=w4s[1][:, a, 512 * c - scuts[1] : 512 * c + 512 - scuts[1]],
                         start=(a == 0),
                         stop=(a == 1),
@@ -280,8 +321,44 @@ def tile_prefix_tuning_kv_s11_kernel(
 
         def lace_m(g, c):
             nc.vector.tensor_copy(
-                out=mx[g][c][:].rearrange("p u (x i) t -> p (u x) t i", i=4),
+                out=mx[g][c][:].rearrange("p (x i t) -> p x t i", i=4, t=4),
                 in_=wb0[1][:].rearrange("p t (x i) -> p x t i", i=4),
+            )
+
+        def pair_bank(g, c, q, v):
+            b = bank()
+            n = 512 * c + 256 * q - scuts[c // 2]
+            for e in range(2):
+                t = 2 * v + e
+                for a in range(2):
+                    nc.tensor.matmul_mx(
+                        out=b[:, 256 * e : 256 * e + 256],
+                        lhsT=wuq[g][t][:, 128 * a : 128 * a + 128].bitcast(FP8X4),
+                        lhsT_scale=wus[g][t][:, 128 * a : 128 * a + 128],
+                        rhs=w4[c][a][:, 512 * q : 512 * q + 512].bitcast(FP4X4),
+                        rhs_scale=w4s[c // 2][:, a, n : n + 256],
+                        start=(a == 0),
+                        stop=(a == 1),
+                    )
+            return b
+
+        def drain_pair(park, q, v, b, eng):
+            planes = park[:].rearrange("p (v r) n -> p v (r n)", v=2)
+            copy_out(
+                eng,
+                planes[:, v, 512 * q : 512 * q + 512].rearrange("p (n e) -> p n e", e=2),
+                b[:].rearrange("p (e n) -> p n e", e=2),
+            )
+
+        def pair_units(g, c, park):
+            for q in range(2):
+                for v in range(2):
+                    drain_pair(park, q, v, pair_bank(g, c, q, v), "S")
+
+        def join_m(g, c, park):
+            nc.vector.tensor_copy(
+                out=mx[g][c][:].bitcast(F32).rearrange("p (n v) -> p n v", v=2),
+                in_=park[:].rearrange("p t n -> p (t n)").bitcast(F32).rearrange("p (v n) -> p n v", v=2),
             )
 
         def units(g, u0, u1, engs):
@@ -310,6 +387,7 @@ def tile_prefix_tuning_kv_s11_kernel(
         for i in range(2):
             nc.vector.memset(w4s[i][:].rearrange("p a n -> p (a n)").bitcast(I32), 0)
 
+        nc.vector.tensor_copy(out=ident[:], in_=ident_bf[:])
         load_wu(0, 0)
         load_wu(0, 1)
         load_wu(0, 2)
@@ -324,29 +402,26 @@ def tile_prefix_tuning_kv_s11_kernel(
         load_w4(2)
         for t in range(4):
             load_wu(1, t)
-        load_wi(1, 0, 4)
+        nc.sync.dma_start(out=wi_late[:], in_=wi_src[1])
         load_w4(3)
         for r in range(4):
             load_c(r)
         nc.sync.dma_start(out=bcol[:], in_=bias.rearrange("(g p t) -> p g t", p=P, t=4))
         nc.sync.dma_start(out=gcol[:], in_=gain.rearrange("(g p t) -> p g t", p=P, t=4))
 
-        warm(4)
-        drain_wu(0, 0, turn_split(split(wu_raw[0][0])), "S")
-        warm(2)
-        words = split(wu_raw[0][1])
-        drain_half(1, 0, turn_half(words, 0), "S")
-        second = turn_half(words, 1)
-        drain_wu(0, 2, turn_split(split(wu_raw[0][2])), "S")
-        words = split(wu_raw[0][3])
-        fourth = turn_half(words, 0)
-        drain_half(3, 1, turn_half(words, 1), "S")
+        warm(3)
+        drain_plain(0, 0, turn_plain(0, 0), "S")
+        drain_plain(0, 1, turn_plain(0, 1), "V")
+        drain_plain(1, 0, turn_plain(1, 0), "S")
+        drain_plain(1, 1, turn_plain(1, 1), "V")
         quant_wu(0, 0)
-        drain_half(1, 1, second, "V")
+        for a in range(2):
+            drain_plain(2, a, turn_plain(2, a), "S")
         quant_wu(0, 1)
-        drain_half(3, 0, fourth, "V")
-        for t in (2, 3):
-            quant_wu(0, t)
+        drain_plain(3, 0, turn_plain(3, 0), "V")
+        drain_plain(3, 1, turn_plain(3, 1), "S")
+        quant_wu(0, 2)
+        quant_wu(0, 3)
         for t in (0, 2, 3):
             widen_half(t, 0, "V")
         widen_half(0, 1, "V")

@@ -44,8 +44,8 @@ def tile_prefix_tuning_kv_s11_kernel(
         wux = [[sb("wux%d%d" % (g, t), [P, 2, 128, 4], BF16) for t in range(4)] for g in range(2)]
         wuq = [[sb("wuq%d%d" % (g, t), [P, 256], U32) for t in range(4)] for g in range(2)]
         wus = [[sb("wus%d%d" % (g, t), [P, 256], U8) for t in range(4)] for g in range(2)]
-        w4_rest = [sb("w4_%d" % c, [P, 2, 1024], U8) for c in range(4)]
-        w4 = [[x[:, a, :] for a in range(2)] for x in w4_rest]
+        w4_rest = [sb("w4_%d" % c, [P, 2, 1024], U8) for c in range(1, 4)]
+        w4 = [[sb("w4_0%d" % a, [P, 1024], U8) for a in range(2)]] + [[x[:, a, :] for a in range(2)] for x in w4_rest]
         scuts = (0, 1024, N)
         w4s = [sb("w4s_%d" % i, [P, 2, scuts[i + 1] - scuts[i]], U8) for i in range(2)]
         craw = [sb("craw%d" % r, [P, K], BF16) for r in range(4)]
@@ -88,7 +88,7 @@ def tile_prefix_tuning_kv_s11_kernel(
 
         def load_w4(c):
             nc.sync.dma_start(
-                out=w4_rest[c][:].bitcast(I32),
+                out=w4_rest[c - 1][:].bitcast(I32),
                 in_=wkv_words.rearrange("g p b -> p g b")[:, :, 1024 * c : 1024 * c + 1024].bitcast(I32),
             )
 
@@ -257,6 +257,9 @@ def tile_prefix_tuning_kv_s11_kernel(
                         start=(g == 0),
                         stop=(g == 1),
                     )
+            return b
+
+        def squash(s, h, v, b):
             for e in range(2):
                 t = 2 * v + e
                 nc.scalar.activation(
@@ -305,6 +308,7 @@ def tile_prefix_tuning_kv_s11_kernel(
             nc.sync.dma_start(out=dst, in_=y[:])
 
         def wide_units(g, c, engs):
+            done = []
             for t in range(4):
                 b = bank()
                 for a in range(2):
@@ -317,7 +321,16 @@ def tile_prefix_tuning_kv_s11_kernel(
                         start=(a == 0),
                         stop=(a == 1),
                     )
-                copy_out(engs[t], wb0[1][:, t, :], b[:])
+                done.append(b)
+                if t % 2 == 1:
+                    copy_out(engs[t], wb0[1][:, t, :], done[t][:])
+                    copy_out(engs[t - 1], wb0[1][:, t - 1, :], done[t - 1][:])
+
+        def units_two(g, u0, u1):
+            for u in range(u0, u1, 2):
+                pair = [unit(g, u), unit(g, u + 1)]
+                drain_m(g, u + 1, pair[1], "S")
+                drain_m(g, u, pair[0], "S")
 
         def lace_m(g, c):
             nc.vector.tensor_copy(
@@ -366,8 +379,9 @@ def tile_prefix_tuning_kv_s11_kernel(
                 drain_m(g, u, unit_part(g, u, bank(), range(4)), engs[(u - u0) % len(engs)])
 
         def hiddens(s, h):
-            for v in range(2):
-                hidden(s, h, v)
+            pair = [hidden(s, h, v) for v in range(2)]
+            for v in (0, 1):
+                squash(s, h, v, pair[v])
 
         def unit(g, u):
             return unit_part(g, u, bank(), range(4))
@@ -393,9 +407,10 @@ def tile_prefix_tuning_kv_s11_kernel(
         load_wu(0, 2)
         load_wu(0, 3)
         load_w4s(0)
-        load_w4(0)
-        nc.sync.dma_start(out=wisc[:], in_=w_in_scale.rearrange("(g p t) o -> p g (t o)", p=P, t=4))
+        load_w4_pass(0, 0)
+        load_w4_pass(0, 1)
         load_wi(0, 0, 2)
+        nc.sync.dma_start(out=wisc[:], in_=w_in_scale.rearrange("(g p t) o -> p g (t o)", p=P, t=4))
         load_wi(0, 2, 4)
         load_w4(1)
         load_w4s(1)
@@ -432,31 +447,38 @@ def tile_prefix_tuning_kv_s11_kernel(
         for u in range(4):
             b = bank()
             first.append(b)
-        for t in range(4):
+        for a in range(2):
+            for u in range(4):
+                one_pass(0, u, first[u], 0, a)
+        for t in range(1, 4):
             for u in range(4):
                 unit_part(0, u, first[u], [t])
-        for u in range(4):
+        for u in (1, 0, 3, 2):
             drain_m(0, u, first[u], "S")
         lace(0, 0)
-        units(0, 4, 8, "S")
+        units_two(0, 4, 8)
         lace(0, 1)
         held = unit(0, 8)
-        units(0, 9, 12, "S")
+        units_two(0, 9, 11)
+        units(0, 11, 12, "S")
         parts = [split(wu_raw[1][t]) for t in range(4)]
         drain_m(0, 8, held, "V")
-        for t in range(4):
-            drain_wu(1, t, turn_split(parts[t]), "S")
+        turned = [turn_split(x) for x in parts]
+        for t in (1, 0, 3, 2):
+            drain_wu(1, t, turned[t], "S")
         for t in range(4):
             widen(wb1[:, t, :], 1, t, 0, F, "V")
-        wide_units(0, 3, "SSSS")
+        pair_units(0, 3, wb0[1])
         parts = [split(craw[r]) for r in range(4)]
         for t in range(4):
             quant_wu(1, t)
-        for r in range(4):
-            drain_c(r, turn_split(parts[r]), "S")
+        turned = [turn_split(x) for x in parts]
+        for r in (1, 0, 3, 2):
+            drain_c(r, turned[r], "S")
         lace(1, 0)
         lace(1, 1)
-        units(1, 0, 7, "S")
+        units_two(1, 0, 6)
+        units(1, 6, 7, "S")
         held = [unit(1, u) for u in (7, 8)]
         quant_wi(0, 0)
         quant_wi(1, 0)
@@ -471,7 +493,8 @@ def tile_prefix_tuning_kv_s11_kernel(
         for u in (7, 8):
             drain_m(1, u, held[u - 7], "V")
         gains(0, 0)
-        units(1, 9, 12, "S")
+        units_two(1, 9, 11)
+        units(1, 11, 12, "S")
         gains(0, 1)
         quant_h(0, 0)
         quant_h(0, 1)
@@ -482,24 +505,27 @@ def tile_prefix_tuning_kv_s11_kernel(
         quant_m(0, 8, 12)
         gains(1, 0)
         finals(0, 0, "SS")
-        units(1, 12, 13, "S")
+        held = unit(1, 12)
         quant_m(1, 8, 12)
         gains(1, 1)
         quant_h(1, 0)
         quant_h(1, 1)
-        lace_m(0, 3)
         finals(0, 1, "SS")
-        units(1, 13, 14, "S")
-        finals(0, 2, "SS")
-        units(1, 14, 15, "S")
-        quant_m(1, 12, 14)
+        drain_m(1, 12, held, "S")
+        held = unit(1, 13)
+        join_m(0, 3, wb0[1])
+        finals(0, 2, "SV")
+        drain_m(1, 13, held, "S")
         quant_m(0, 12, 16)
-        finals(1, 0, "SV")
+        held = unit(1, 14)
+        finals(1, 0, "SS")
+        drain_m(1, 14, held, "V")
         out_tile(2, 512, 1024, "S")
+        quant_m(1, 12, 14)
         units(1, 15, 16, "V")
         out_twin(3, 512, "SS")
         quant_m(1, 14, 16)
-        out_twin(2, 1024)
+        out_twin(2, 1024, "SS")
         out_twin(3, 1024)
         for i in range(4):
             out_twin(i, 1536)

@@ -34,7 +34,7 @@ def tile_prefix_tuning_kv_s11_kernel(
         def sb(name, shape, dtype):
             return keep.tile(shape, dtype, name=name, align_bytes=64)
 
-        zeros = sb("zeros", [P, 512], BF16)
+        zeros = sb("zeros", [P, P], BF16)
         nc.gpsimd.memset(zeros[:].bitcast(I32), 0)
         ident_bf = sb("ident_bf", [P, P], BF16)
         make_identity(nc, ident_bf[:])
@@ -52,8 +52,7 @@ def tile_prefix_tuning_kv_s11_kernel(
         cg = [sb("cg%d" % s, [P, 2, HALF, 4], BF16) for s in range(2)]
         cq = [sb("cq%d" % s, [P, 2, HALF], U32) for s in range(2)]
         cs = [sb("cs%d" % s, [P, 2, HALF], U8) for s in range(2)]
-        wi_late = sb("wi_late", [P, 4, F], U8)
-        wi = [[sb("wi0%d" % v, [P, 2, F], U8) for v in range(2)], [wi_late[:, 2 * v : 2 * v + 2, :] for v in range(2)]]
+        wi = [[sb("wi%d%d" % (g, v), [P, 2, F], U8) for v in range(2)] for g in range(2)]
         wisc = sb("wisc", [P, 2, 4], F32)
         wb0 = [sb("wb0%d" % h, [P, 4, 512], BF16) for h in range(2)]
         wb1 = sb("wb1", [P, 4, F], BF16)
@@ -374,6 +373,12 @@ def tile_prefix_tuning_kv_s11_kernel(
                 in_=park[:].rearrange("p t n -> p (t n)").bitcast(F32).rearrange("p (v n) -> p n v", v=2),
             )
 
+        def join_half(g, c, park):
+            nc.vector.tensor_copy(
+                out=mx[g][c][:, 1024:2048].bitcast(F32).rearrange("p (n v) -> p n v", v=2),
+                in_=park[:].rearrange("p t n -> p (t n)").bitcast(F32).rearrange("p (v n) -> p n v", v=2)[:, 256:512, :],
+            )
+
         def units(g, u0, u1, engs):
             for u in range(u0, u1):
                 drain_m(g, u, unit_part(g, u, bank(), range(4)), engs[(u - u0) % len(engs)])
@@ -396,7 +401,13 @@ def tile_prefix_tuning_kv_s11_kernel(
         def warm(n):
             b = bank()
             for i in range(n):
-                nc.tensor.matmul(out=b[:], lhsT=zeros[:, 0:128], rhs=zeros[:], start=True, stop=True)
+                nc.tensor.matmul(
+                    out=b[:].rearrange("p (x n) -> p x n", x=4),
+                    lhsT=zeros[:],
+                    rhs=zeros[:].unsqueeze(1).to_broadcast([P, 4, P]),
+                    start=True,
+                    stop=True,
+                )
 
         for i in range(2):
             nc.vector.memset(w4s[i][:].rearrange("p a n -> p (a n)").bitcast(I32), 0)
@@ -417,14 +428,15 @@ def tile_prefix_tuning_kv_s11_kernel(
         load_w4(2)
         for t in range(4):
             load_wu(1, t)
-        nc.sync.dma_start(out=wi_late[:], in_=wi_src[1])
+        load_wi(1, 0, 2)
+        load_wi(1, 2, 4)
         load_w4(3)
         for r in range(4):
             load_c(r)
         nc.sync.dma_start(out=bcol[:], in_=bias.rearrange("(g p t) -> p g t", p=P, t=4))
         nc.sync.dma_start(out=gcol[:], in_=gain.rearrange("(g p t) -> p g t", p=P, t=4))
 
-        warm(3)
+        warm(4)
         drain_plain(0, 0, turn_plain(0, 0), "S")
         drain_plain(0, 1, turn_plain(0, 1), "V")
         drain_plain(1, 0, turn_plain(1, 0), "S")
@@ -459,8 +471,10 @@ def tile_prefix_tuning_kv_s11_kernel(
         units_two(0, 4, 8)
         lace(0, 1)
         held = unit(0, 8)
-        units_two(0, 9, 11)
-        units(0, 11, 12, "S")
+        units(0, 9, 10, "S")
+        both = [pair_bank(0, 2, 1, v) for v in range(2)]
+        for v in (1, 0):
+            drain_pair(wb0[0], 1, v, both[v], "S")
         parts = [split(wu_raw[1][t]) for t in range(4)]
         drain_m(0, 8, held, "V")
         turned = [turn_split(x) for x in parts]
@@ -490,8 +504,9 @@ def tile_prefix_tuning_kv_s11_kernel(
         quant_m(0, 0, 4)
         hiddens(0, 1)
         quant_m(1, 0, 4)
-        for u in (7, 8):
+        for u in (8, 7):
             drain_m(1, u, held[u - 7], "V")
+        join_half(0, 2, wb0[0])
         gains(0, 0)
         units_two(1, 9, 11)
         units(1, 11, 12, "S")

@@ -34,8 +34,6 @@ def tile_prefix_tuning_kv_s11_kernel(
         def sb(name, shape, dtype):
             return keep.tile(shape, dtype, name=name, align_bytes=64)
 
-        zeros = sb("zeros", [P, P], BF16)
-        nc.gpsimd.memset(zeros[:].bitcast(I32), 0)
         ident_bf = sb("ident_bf", [P, P], BF16)
         make_identity(nc, ident_bf[:])
         ident = sb("ident", [P, P], F32)
@@ -398,16 +396,6 @@ def tile_prefix_tuning_kv_s11_kernel(
             for i in range(2):
                 out_tile(2 * s + i, 512 * c, 512 * c + 512, engs[i])
 
-        def warm(n):
-            b = bank()
-            for i in range(n):
-                nc.tensor.matmul(
-                    out=b[:].rearrange("p (x n) -> p x n", x=4),
-                    lhsT=zeros[:],
-                    rhs=zeros[:].unsqueeze(1).to_broadcast([P, 4, P]),
-                    start=True,
-                    stop=True,
-                )
 
         for i in range(2):
             nc.vector.memset(w4s[i][:].rearrange("p a n -> p (a n)").bitcast(I32), 0)
@@ -436,7 +424,6 @@ def tile_prefix_tuning_kv_s11_kernel(
         nc.sync.dma_start(out=bcol[:], in_=bias.rearrange("(g p t) -> p g t", p=P, t=4))
         nc.sync.dma_start(out=gcol[:], in_=gain.rearrange("(g p t) -> p g t", p=P, t=4))
 
-        warm(4)
         drain_plain(0, 0, turn_plain(0, 0), "S")
         drain_plain(0, 1, turn_plain(0, 1), "V")
         drain_plain(1, 0, turn_plain(1, 0), "S")

@@ -29,7 +29,7 @@ def tile_prefix_tuning_kv_s11_kernel(
         keep = ctx.enter_context(tc.tile_pool(name="keep", bufs=1))
         yst = ctx.enter_context(tc.tile_pool(name="yst", bufs=10))
         sst = ctx.enter_context(tc.tile_pool(name="sst", bufs=4))
-        psum = ctx.enter_context(tc.psum_pool(name="psum", bufs=8))
+        psum = ctx.enter_context(tc.psum_pool(name="psum", bufs=1))
 
         def sb(name, shape, dtype):
             return keep.tile(shape, dtype, name=name, align_bytes=64)
@@ -45,7 +45,7 @@ def tile_prefix_tuning_kv_s11_kernel(
         w4_rest = [sb("w4_%d" % c, [P, 2, 1024], U8) for c in range(1, 4)]
         w4 = [[sb("w4_0%d" % a, [P, 1024], U8) for a in range(2)]] + [[x[:, a, :] for a in range(2)] for x in w4_rest]
         scuts = (0, 1024, N)
-        w4s = [sb("w4s_%d" % i, [P, 2, scuts[i + 1] - scuts[i]], U8) for i in range(2)]
+        w4s = [sb("w4s_%d" % i, [P, 2, scuts[i + 1] - scuts[i]], U8) for i in range(len(scuts) - 1)]
         craw = [sb("craw%d" % r, [P, K], BF16) for r in range(4)]
         cg = [sb("cg%d" % s, [P, 2, HALF, 4], BF16) for s in range(2)]
         cq = [sb("cq%d" % s, [P, 2, HALF], U32) for s in range(2)]
@@ -94,6 +94,9 @@ def tile_prefix_tuning_kv_s11_kernel(
                 out=w4[c][a][:].bitcast(I32), in_=wkv_words[a][:, 1024 * c : 1024 * c + 1024].bitcast(I32)
             )
 
+        def load_wisc():
+            nc.sync.dma_start(out=wisc[:], in_=w_in_scale.rearrange("(g p t) o -> p g (t o)", p=P, t=4))
+
         def load_w4s(i):
             for q in range(4):
                 nc.sync.dma_start(
@@ -103,18 +106,32 @@ def tile_prefix_tuning_kv_s11_kernel(
                     .bitcast(I32),
                 )
 
+        def w_scale(a, n0, n1):
+            j = max(i for i in range(len(scuts) - 1) if scuts[i] <= n0)
+            return w4s[j][:, a, n0 - scuts[j] : n1 - scuts[j]]
+
         def copy_out(eng, out, in_):
             if eng == "S":
                 nc.scalar.copy(out=out, in_=in_)
             else:
                 nc.vector.tensor_copy(out=out, in_=in_)
 
+        free, taken, live, take = list(range(8)), [], [], [2]
+
         def bank():
-            b = psum.tile([P, 512], F32, name="bank", tag="bank")
+            if not taken:
+                taken.extend(free[: take[0]])
+                free[: take[0]] = []
+            i = taken.pop()
+            b = psum.tile([P, 512], F32, name="bank%d" % i, tag="bank%d" % i)
+            live.append((b, i))
             return b
 
-        def split(raw, spare=None):
-            x = sst.tile([P, 512], F32, name="split", tag="split", align_bytes=64) if spare is None else spare[:].bitcast(F32)
+        def release(b):
+            free.append([i for x, i in live if x is b][0])
+
+        def split(raw):
+            x = sst.tile([P, 512], F32, name="split", tag="split", align_bytes=64)
             nc.vector.tensor_copy(
                 out=x[:].rearrange("p (a u c i) -> p a c u i", a=2, u=2, i=4),
                 in_=raw[:].bitcast(F32).rearrange("p (a c i u) -> p a c u i", a=2, u=2, i=4),
@@ -141,19 +158,11 @@ def tile_prefix_tuning_kv_s11_kernel(
 
         def drain_plain(t, a, b, eng):
             copy_out(eng, wux[0][t][:, a], b[:].rearrange("p (j r) -> p r j", j=4))
-
-        def turn_half(x, a):
-            b = bank()
-            for u in range(2):
-                i = 2 * a + u
-                nc.tensor.transpose(b[:, 128 * u : 128 * u + 128], x[:, 128 * i : 128 * i + 128], ident[:])
-            return b
-
-        def drain_half(t, a, b, eng):
-            copy_out(eng, wux[0][t][:, a].bitcast(F32), b[:, 0:256].rearrange("p (u r) -> p r u", u=2))
+            release(b)
 
         def drain_wu(g, t, b, eng):
             copy_out(eng, wux[g][t][:].bitcast(F32), b[:].rearrange("p (a u r) -> p a r u", a=2, u=2))
+            release(b)
 
         def quant_wu(g, t):
             nc.vector.quantize_mx(
@@ -168,6 +177,7 @@ def tile_prefix_tuning_kv_s11_kernel(
                 cg[r // 2][:, :, 128 * (r % 2) : 128 * (r % 2) + 128, :].bitcast(F32),
                 b[:].rearrange("p (a u r) -> p a r u", a=2, u=2),
             )
+            release(b)
 
         def quant_c(s):
             nc.vector.quantize_mx(
@@ -186,8 +196,8 @@ def tile_prefix_tuning_kv_s11_kernel(
         def widen_half(t, h, eng):
             widen(wb0[h][:, t, :], 0, t, 512 * h, 512 * h + 512, eng)
 
-        def widen_late(t, h, eng="V"):
-            widen(wb1[:, t, 512 * h : 512 * h + 512], 1, t, 512 * h, 512 * h + 512, eng)
+        def widen_row(t):
+            widen(wb1[:, t, :], 1, t, 0, F, "V")
 
         def lace(g, h):
             rows = wb0[h][:] if g == 0 else wb1[:, :, 512 * h : 512 * h + 512]
@@ -196,48 +206,88 @@ def tile_prefix_tuning_kv_s11_kernel(
                 in_=rows.rearrange("p j (m t) -> p m j t", t=4),
             )
 
-        def quant_wi(g, h):
-            nc.vector.quantize_mx(out=wq[g][h][:].bitcast(FP8X4), scales=ws[g][h][:], in_=wg[g][h][:])
+        def quant_wi(g, h, t0=0, t1=4):
+            nc.vector.quantize_mx(
+                out=wq[g][h][:, 128 * t0 : 128 * t1].bitcast(FP8X4),
+                scales=ws[g][h][:, 128 * t0 : 128 * t1],
+                in_=wg[g][h][:, 512 * t0 : 512 * t1],
+            )
 
-        def unit_part(g, u, b, ts):
-            n = 128 * (u % 4)
-            j = u // 8
-            m = 128 * u - scuts[j]
-            for t in ts:
-                for a in range(2):
-                    nc.tensor.matmul_mx(
-                        out=b[:, 128 * t : 128 * t + 128],
-                        lhsT=wuq[g][t][:, 128 * a : 128 * a + 128].bitcast(FP8X4),
-                        lhsT_scale=wus[g][t][:, 128 * a : 128 * a + 128],
-                        rhs=w4[u // 4][a][:, 2 * n : 2 * n + 256].bitcast(FP4X4),
-                        rhs_scale=w4s[j][:, a, m : m + 128],
-                        start=(a == 0),
-                        stop=(a == 1),
-                    )
-            return b
-
-        def one_pass(g, u, b, t, a):
-            n = 128 * (u % 4)
-            j = u // 8
-            m = 128 * u - scuts[j]
+        def m_pass(out, g, t, a, n0, n1):
+            c = n0 // 512
             nc.tensor.matmul_mx(
-                out=b[:, 128 * t : 128 * t + 128],
+                out=out,
                 lhsT=wuq[g][t][:, 128 * a : 128 * a + 128].bitcast(FP8X4),
                 lhsT_scale=wus[g][t][:, 128 * a : 128 * a + 128],
-                rhs=w4[u // 4][a][:, 2 * n : 2 * n + 256].bitcast(FP4X4),
-                rhs_scale=w4s[j][:, a, m : m + 128],
+                rhs=w4[c][a][:, 2 * (n0 - 512 * c) : 2 * (n1 - 512 * c)].bitcast(FP4X4),
+                rhs_scale=w_scale(a, n0, n1),
                 start=(a == 0),
                 stop=(a == 1),
             )
 
+        def one_pass(g, u, b, t, a):
+            m_pass(b[:, 128 * t : 128 * t + 128], g, t, a, 128 * u, 128 * u + 128)
+
+        def unit_part(g, u, b, ts):
+            for t in ts:
+                for a in range(2):
+                    one_pass(g, u, b, t, a)
+            return b
+
+        def unit(g, u):
+            return unit_part(g, u, bank(), range(4))
+
         def drain_m(g, u, b, eng):
-            copy_out(eng, mx[g][u // 4][:, 512 * (u % 4) : 512 * (u % 4) + 512].rearrange("p (n t) -> p n t", t=4), b[:].rearrange("p (t n) -> p n t", t=4))
+            copy_out(
+                eng,
+                mx[g][u // 4][:, 512 * (u % 4) : 512 * (u % 4) + 512].rearrange("p (n t) -> p n t", t=4),
+                b[:].rearrange("p (t n) -> p n t", t=4),
+            )
+            release(b)
+
+        def units(g, u0, u1, eng):
+            for u in range(u0, u1):
+                drain_m(g, u, unit(g, u), eng)
+
+        def units_two(g, u0, u1):
+            for u in range(u0, u1, 2):
+                pair = [unit(g, u), unit(g, u + 1)]
+                drain_m(g, u + 1, pair[1], "S")
+                drain_m(g, u, pair[0], "S")
 
         def quant_m(g, u0, u1):
             nc.vector.quantize_mx(
                 out=mq[g][:, 128 * u0 : 128 * u1].bitcast(FP8X4),
                 scales=ms[g][:, 128 * u0 : 128 * u1],
                 in_=mx[g][u0 // 4][:, 512 * (u0 % 4) : 512 * ((u1 - 1) % 4 + 1)],
+            )
+
+        def pair_bank(g, c, q, v):
+            b = bank()
+            n = 512 * c + 256 * q
+            for e in range(2):
+                for a in range(2):
+                    m_pass(b[:, 256 * e : 256 * e + 256], g, 2 * v + e, a, n, n + 256)
+            return b
+
+        def drain_pair(park, q, v, b, eng):
+            planes = park[:].rearrange("p (v r) n -> p v (r n)", v=2)
+            copy_out(
+                eng,
+                planes[:, v, 512 * q : 512 * q + 512].rearrange("p (n e) -> p n e", e=2),
+                b[:].rearrange("p (e n) -> p n e", e=2),
+            )
+            release(b)
+
+        def pair_half(g, c, q, park, order=(0, 1), engs="SS"):
+            both = [pair_bank(g, c, q, v) for v in range(2)]
+            for v in order:
+                drain_pair(park, q, v, both[v], engs[v])
+
+        def join(g, c, park, q0, q1):
+            nc.vector.tensor_copy(
+                out=mx[g][c][:, 1024 * q0 : 1024 * q1].bitcast(F32).rearrange("p (n v) -> p n v", v=2),
+                in_=park[:].rearrange("p t n -> p (t n)").bitcast(F32).rearrange("p (v n) -> p n v", v=2)[:, 256 * q0 : 256 * q1, :],
             )
 
         def hidden(s, h, v):
@@ -262,6 +312,12 @@ def tile_prefix_tuning_kv_s11_kernel(
                 nc.scalar.activation(
                     out=th[s][h][:, t, :], in_=b[:, HALF * e : HALF * e + HALF], func=TANH, bias=bcol[:, h, t : t + 1]
                 )
+            release(b)
+
+        def hiddens(s, h):
+            pair = [hidden(s, h, v) for v in range(2)]
+            for v in (0, 1):
+                squash(s, h, v, pair[v])
 
         def gains(s, h):
             nc.vector.tensor_tensor(
@@ -290,126 +346,45 @@ def tile_prefix_tuning_kv_s11_kernel(
                 )
             return b
 
-        def drain_y(i, n0, n1, b, eng):
-            y = yst.tile([P, 512], F32, name="y", tag="y", align_bytes=64)
-            dst = outs[n0 // 1024][i // 2][i % 2][:, n0 % 1024 : n0 % 1024 + n1 - n0]
-            copy_out(eng, y[:, 0 : n1 - n0], b[:, 0 : n1 - n0])
-            nc.sync.dma_start(out=dst, in_=y[:, 0 : n1 - n0])
+        def store(i, n0, y):
+            nc.sync.dma_start(out=outs[n0 // 1024][i // 2][i % 2][:, n0 % 1024 : n0 % 1024 + 512], in_=y[:])
 
-        def out_twin(i, n0, engs="VS"):
+        def drain_y(i, n0, b, eng):
+            y = yst.tile([P, 512], F32, name="y", tag="y", align_bytes=64)
+            copy_out(eng, y[:], b[:])
+            release(b)
+            store(i, n0, y)
+
+        def out_tile(i, n0, eng):
+            drain_y(i, n0, final(i, n0, n0 + 512), eng)
+
+        def finals_last(s, c):
+            done = [final(2 * s + i, 512 * c, 512 * c + 512) for i in range(2)]
+            for i in (1, 0):
+                drain_y(2 * s + i, 512 * c, done[i], "S")
+
+        def out_twin(i, n0, engs):
             y = yst.tile([P, 512], F32, name="y", tag="y", align_bytes=64)
             for e in range(2):
                 b = final(i, n0 + 256 * e, n0 + 256 * e + 256)
                 copy_out(engs[e], y[:, 256 * e : 256 * e + 256], b[:, 0:256])
-            dst = outs[n0 // 1024][i // 2][i % 2][:, n0 % 1024 : n0 % 1024 + 512]
-            nc.sync.dma_start(out=dst, in_=y[:])
-
-        def wide_units(g, c, engs):
-            done = []
-            for t in range(4):
-                b = bank()
-                for a in range(2):
-                    nc.tensor.matmul_mx(
-                        out=b[:],
-                        lhsT=wuq[g][t][:, 128 * a : 128 * a + 128].bitcast(FP8X4),
-                        lhsT_scale=wus[g][t][:, 128 * a : 128 * a + 128],
-                        rhs=w4[c][a][:].bitcast(FP4X4),
-                        rhs_scale=w4s[1][:, a, 512 * c - scuts[1] : 512 * c + 512 - scuts[1]],
-                        start=(a == 0),
-                        stop=(a == 1),
-                    )
-                done.append(b)
-                if t % 2 == 1:
-                    copy_out(engs[t], wb0[1][:, t, :], done[t][:])
-                    copy_out(engs[t - 1], wb0[1][:, t - 1, :], done[t - 1][:])
-
-        def units_two(g, u0, u1):
-            for u in range(u0, u1, 2):
-                pair = [unit(g, u), unit(g, u + 1)]
-                drain_m(g, u + 1, pair[1], "S")
-                drain_m(g, u, pair[0], "S")
-
-        def lace_m(g, c):
-            nc.vector.tensor_copy(
-                out=mx[g][c][:].rearrange("p (x i t) -> p x t i", i=4, t=4),
-                in_=wb0[1][:].rearrange("p t (x i) -> p x t i", i=4),
-            )
-
-        def pair_bank(g, c, q, v):
-            b = bank()
-            n = 512 * c + 256 * q - scuts[c // 2]
-            for e in range(2):
-                t = 2 * v + e
-                for a in range(2):
-                    nc.tensor.matmul_mx(
-                        out=b[:, 256 * e : 256 * e + 256],
-                        lhsT=wuq[g][t][:, 128 * a : 128 * a + 128].bitcast(FP8X4),
-                        lhsT_scale=wus[g][t][:, 128 * a : 128 * a + 128],
-                        rhs=w4[c][a][:, 512 * q : 512 * q + 512].bitcast(FP4X4),
-                        rhs_scale=w4s[c // 2][:, a, n : n + 256],
-                        start=(a == 0),
-                        stop=(a == 1),
-                    )
-            return b
-
-        def drain_pair(park, q, v, b, eng):
-            planes = park[:].rearrange("p (v r) n -> p v (r n)", v=2)
-            copy_out(
-                eng,
-                planes[:, v, 512 * q : 512 * q + 512].rearrange("p (n e) -> p n e", e=2),
-                b[:].rearrange("p (e n) -> p n e", e=2),
-            )
-
-        def pair_units(g, c, park):
-            for q in range(2):
-                for v in range(2):
-                    drain_pair(park, q, v, pair_bank(g, c, q, v), "S")
-
-        def join_m(g, c, park):
-            nc.vector.tensor_copy(
-                out=mx[g][c][:].bitcast(F32).rearrange("p (n v) -> p n v", v=2),
-                in_=park[:].rearrange("p t n -> p (t n)").bitcast(F32).rearrange("p (v n) -> p n v", v=2),
-            )
-
-        def join_half(g, c, park):
-            nc.vector.tensor_copy(
-                out=mx[g][c][:, 1024:2048].bitcast(F32).rearrange("p (n v) -> p n v", v=2),
-                in_=park[:].rearrange("p t n -> p (t n)").bitcast(F32).rearrange("p (v n) -> p n v", v=2)[:, 256:512, :],
-            )
-
-        def units(g, u0, u1, engs):
-            for u in range(u0, u1):
-                drain_m(g, u, unit_part(g, u, bank(), range(4)), engs[(u - u0) % len(engs)])
-
-        def hiddens(s, h):
-            pair = [hidden(s, h, v) for v in range(2)]
-            for v in (0, 1):
-                squash(s, h, v, pair[v])
-
-        def unit(g, u):
-            return unit_part(g, u, bank(), range(4))
-
-        def out_tile(i, n0, n1, eng):
-            drain_y(i, n0, n1, final(i, n0, n1), eng)
+                release(b)
+            store(i, n0, y)
 
         def finals(s, c, engs):
             for i in range(2):
-                out_tile(2 * s + i, 512 * c, 512 * c + 512, engs[i])
+                out_tile(2 * s + i, 512 * c, engs[i])
 
-
-        for i in range(2):
-            nc.vector.memset(w4s[i][:].rearrange("p a n -> p (a n)").bitcast(I32), 0)
-
+        for x in w4s:
+            nc.vector.memset(x[:].rearrange("p a n -> p (a n)").bitcast(I32), 0)
         nc.vector.tensor_copy(out=ident[:], in_=ident_bf[:])
-        load_wu(0, 0)
-        load_wu(0, 1)
-        load_wu(0, 2)
-        load_wu(0, 3)
+        for t in range(4):
+            load_wu(0, t)
         load_w4s(0)
         load_w4_pass(0, 0)
         load_w4_pass(0, 1)
         load_wi(0, 0, 2)
-        nc.sync.dma_start(out=wisc[:], in_=w_in_scale.rearrange("(g p t) o -> p g (t o)", p=P, t=4))
+        load_wisc()
         load_wi(0, 2, 4)
         load_w4(1)
         load_w4s(1)
@@ -457,19 +432,19 @@ def tile_prefix_tuning_kv_s11_kernel(
         lace(0, 0)
         units_two(0, 4, 8)
         lace(0, 1)
+        take[0] = 1
         held = unit(0, 8)
         units(0, 9, 10, "S")
-        both = [pair_bank(0, 2, 1, v) for v in range(2)]
-        for v in (1, 0):
-            drain_pair(wb0[0], 1, v, both[v], "S")
+        pair_half(0, 2, 1, wb0[0], (1, 0))
         parts = [split(wu_raw[1][t]) for t in range(4)]
         drain_m(0, 8, held, "V")
         turned = [turn_split(x) for x in parts]
         for t in (1, 0, 3, 2):
             drain_wu(1, t, turned[t], "S")
         for t in range(4):
-            widen(wb1[:, t, :], 1, t, 0, F, "V")
-        pair_units(0, 3, wb0[1])
+            widen_row(t)
+        for q in range(2):
+            pair_half(0, 3, q, wb0[1], (1, 0))
         parts = [split(craw[r]) for r in range(4)]
         for t in range(4):
             quant_wu(1, t)
@@ -493,8 +468,9 @@ def tile_prefix_tuning_kv_s11_kernel(
         quant_m(1, 0, 4)
         for u in (8, 7):
             drain_m(1, u, held[u - 7], "V")
-        join_half(0, 2, wb0[0])
+        join(0, 2, wb0[0], 1, 2)
         gains(0, 0)
+        take[0] = 2
         units_two(1, 9, 11)
         units(1, 11, 12, "S")
         gains(0, 1)
@@ -506,28 +482,28 @@ def tile_prefix_tuning_kv_s11_kernel(
         hiddens(1, 1)
         quant_m(0, 8, 12)
         gains(1, 0)
-        finals(0, 0, "SS")
+        finals_last(0, 0)
         held = unit(1, 12)
         quant_m(1, 8, 12)
         gains(1, 1)
         quant_h(1, 0)
         quant_h(1, 1)
-        finals(0, 1, "SS")
+        finals_last(0, 1)
         drain_m(1, 12, held, "S")
         held = unit(1, 13)
-        join_m(0, 3, wb0[1])
+        join(0, 3, wb0[1], 0, 2)
         finals(0, 2, "SV")
         drain_m(1, 13, held, "S")
         quant_m(0, 12, 16)
         held = unit(1, 14)
         finals(1, 0, "SS")
         drain_m(1, 14, held, "V")
-        out_tile(2, 512, 1024, "S")
+        out_tile(2, 512, "S")
         quant_m(1, 12, 14)
         units(1, 15, 16, "V")
         out_twin(3, 512, "SS")
         quant_m(1, 14, 16)
         out_twin(2, 1024, "SS")
-        out_twin(3, 1024)
+        out_twin(3, 1024, "VS")
         for i in range(4):
-            out_twin(i, 1536)
+            out_twin(i, 1536, "VS")

from contextlib import ExitStack

import concourse.mybir as mybir
from concourse.masks import make_identity

P = 128
ROWS, K, F, D, N = 512, 1024, 1024, 1024, 2048
HALF = ROWS // 2
FLOPS = 2 * (ROWS * K * F + F * D * N + ROWS * F * N)

F32 = mybir.dt.float32
BF16 = mybir.dt.bfloat16
I32 = mybir.dt.int32
U32 = mybir.dt.uint32
U8 = mybir.dt.uint8
FP8 = mybir.dt.float8_e4m3fn
FP8X4 = mybir.dt.float8_e4m3fn_x4
FP4X4 = mybir.dt.float4_e2m1fn_x4
MULT = mybir.AluOpType.mult
COPY = mybir.ActivationFunctionType.Copy
TANH = mybir.ActivationFunctionType.Tanh


def tile_prefix_tuning_kv_s11_kernel(
    tc, codes, w_in_bytes, w_in_scale, bias, gain, w_up, wkv_words, wkv_scales, keys, values
):
    nc = tc.nc
    with ExitStack() as ctx:
        keep = ctx.enter_context(tc.tile_pool(name="keep", bufs=1))
        yst = ctx.enter_context(tc.tile_pool(name="yst", bufs=10))
        sst = ctx.enter_context(tc.tile_pool(name="sst", bufs=4))
        psum = ctx.enter_context(tc.psum_pool(name="psum", bufs=1))

        def sb(name, shape, dtype):
            return keep.tile(shape, dtype, name=name, align_bytes=64)

        ident_bf = sb("ident_bf", [P, P], BF16)
        make_identity(nc, ident_bf[:])
        ident = sb("ident", [P, P], F32)

        wu_raw = [[sb("wu_raw%d%d" % (g, t), [P, D], BF16) for t in range(4)] for g in range(2)]
        wux = [[sb("wux%d%d" % (g, t), [P, 2, 128, 4], BF16) for t in range(4)] for g in range(2)]
        wuq = [[sb("wuq%d%d" % (g, t), [P, 256], U32) for t in range(4)] for g in range(2)]
        wus = [[sb("wus%d%d" % (g, t), [P, 256], U8) for t in range(4)] for g in range(2)]
        w4_rest = [sb("w4_%d" % c, [P, 2, 1024], U8) for c in range(1, 4)]
        w4 = [[sb("w4_0%d" % a, [P, 1024], U8) for a in range(2)]] + [[x[:, a, :] for a in range(2)] for x in w4_rest]
        scuts = (0, 1024, N)
        w4s = [sb("w4s_%d" % i, [P, 2, scuts[i + 1] - scuts[i]], U8) for i in range(len(scuts) - 1)]
        craw = [sb("craw%d" % r, [P, K], BF16) for r in range(4)]
        cg = [sb("cg%d" % s, [P, 2, HALF, 4], BF16) for s in range(2)]
        cq = [sb("cq%d" % s, [P, 2, HALF], U32) for s in range(2)]
        cs = [sb("cs%d" % s, [P, 2, HALF], U8) for s in range(2)]
        wi = [[sb("wi%d%d" % (g, v), [P, 2, F], U8) for v in range(2)] for g in range(2)]
        wisc = sb("wisc", [P, 2, 4], F32)
        wb0 = [sb("wb0%d" % h, [P, 4, 512], BF16) for h in range(2)]
        wb1 = sb("wb1", [P, 4, F], BF16)
        wg = [[sb("wg%d%d" % (g, h), [P, 2048], BF16) for h in range(2)] for g in range(2)]
        wq = [[sb("wq%d%d" % (g, h), [P, 512], U32) for h in range(2)] for g in range(2)]
        ws = [[sb("ws%d%d" % (g, h), [P, 512], U8) for h in range(2)] for g in range(2)]
        bcol = sb("bcol", [P, 2, 4], BF16)
        gcol = sb("gcol", [P, 2, 4], BF16)
        th = [[sb("th%d%d" % (s, g), [P, 4, HALF], F32) for g in range(2)] for s in range(2)]
        hg = [[sb("hg%d%d" % (s, h), [P, HALF, 4], BF16) for h in range(2)] for s in range(2)]
        hq = [[sb("hq%d%d" % (s, h), [P, HALF], U32) for h in range(2)] for s in range(2)]
        hs = [[sb("hs%d%d" % (s, h), [P, HALF], U8) for h in range(2)] for s in range(2)]
        mx = [[sb("mx%d%d" % (g, c), [P, 2048], BF16) for c in range(4)] for g in range(2)]
        mq = [sb("mq%d" % g, [P, N], U32) for g in range(2)]
        ms = [sb("ms%d" % g, [P, N], U8) for g in range(2)]

        ctx.enter_context(tc.manual_schedule())

        wu_src = w_up.rearrange("(g p t) d -> g t p d", p=P, t=4)
        wi_src = w_in_bytes.rearrange("(g p t) f -> g p t f", p=P, t=4)
        c_src = codes.rearrange("(r p) k -> r p k", p=P)
        outs = [o.rearrange("(s e p) n -> s e p n", p=P, e=2) for o in (keys, values)]

        def load_wu(g, t):
            nc.sync.dma_start(out=wu_raw[g][t][:], in_=wu_src[g][t])

        def load_c(r):
            nc.sync.dma_start(out=craw[r][:], in_=c_src[r])

        def load_wi(g, t0, t1):
            nc.sync.dma_start(out=wi[g][t0 // 2][:], in_=wi_src[g][:, t0:t1, :])

        def load_w4(c):
            nc.sync.dma_start(
                out=w4_rest[c - 1][:].bitcast(I32),
                in_=wkv_words.rearrange("g p b -> p g b")[:, :, 1024 * c : 1024 * c + 1024].bitcast(I32),
            )

        def load_w4_pass(c, a):
            nc.sync.dma_start(
                out=w4[c][a][:].bitcast(I32), in_=wkv_words[a][:, 1024 * c : 1024 * c + 1024].bitcast(I32)
            )

        def load_wisc():
            nc.sync.dma_start(out=wisc[:], in_=w_in_scale.rearrange("(g p t) o -> p g (t o)", p=P, t=4))

        def load_w4s(i):
            for q in range(4):
                nc.sync.dma_start(
                    out=w4s[i][32 * q : 32 * q + 4, :, :].bitcast(I32),
                    in_=wkv_scales[:, 4 * q : 4 * q + 4, scuts[i] : scuts[i + 1]]
                    .rearrange("g r n -> r g n")
                    .bitcast(I32),
                )

        def w_scale(a, n0, n1):
            j = max(i for i in range(len(scuts) - 1) if scuts[i] <= n0)
            return w4s[j][:, a, n0 - scuts[j] : n1 - scuts[j]]

        def copy_out(eng, out, in_):
            if eng == "S":
                nc.scalar.copy(out=out, in_=in_)
            else:
                nc.vector.tensor_copy(out=out, in_=in_)

        free, taken, live, take = list(range(8)), [], [], [2]

        def bank():
            if not taken:
                taken.extend(free[: take[0]])
                free[: take[0]] = []
            i = taken.pop()
            b = psum.tile([P, 512], F32, name="bank%d" % i, tag="bank%d" % i)
            live.append((b, i))
            return b

        def release(b):
            free.append([i for x, i in live if x is b][0])

        def split(raw):
            x = sst.tile([P, 512], F32, name="split", tag="split", align_bytes=64)
            nc.vector.tensor_copy(
                out=x[:].rearrange("p (a u c i) -> p a c u i", a=2, u=2, i=4),
                in_=raw[:].bitcast(F32).rearrange("p (a c i u) -> p a c u i", a=2, u=2, i=4),
            )
            return x

        def turn_split(x):
            b = bank()
            for i in range(4):
                nc.tensor.transpose(b[:, 128 * i : 128 * i + 128], x[:, 128 * i : 128 * i + 128], ident[:])
            return b

        def turn_plain(t, a):
            b = bank()
            for j in range(4):
                nc.tensor.matmul(
                    out=b[:, 128 * j : 128 * j + 128],
                    lhsT=wu_raw[0][t][:, 512 * a + j : 512 * a + 512 : 4],
                    rhs=ident_bf[:],
                    start=True,
                    stop=True,
                )
            return b

        def drain_plain(t, a, b, eng):
            copy_out(eng, wux[0][t][:, a], b[:].rearrange("p (j r) -> p r j", j=4))
            release(b)

        def drain_wu(g, t, b, eng):
            copy_out(eng, wux[g][t][:].bitcast(F32), b[:].rearrange("p (a u r) -> p a r u", a=2, u=2))
            release(b)

        def quant_wu(g, t):
            nc.vector.quantize_mx(
                out=wuq[g][t][:].bitcast(FP8X4),
                scales=wus[g][t][:],
                in_=wux[g][t][:].rearrange("p a r j -> p (a r j)"),
            )

        def drain_c(r, b, eng):
            copy_out(
                eng,
                cg[r // 2][:, :, 128 * (r % 2) : 128 * (r % 2) + 128, :].bitcast(F32),
                b[:].rearrange("p (a u r) -> p a r u", a=2, u=2),
            )
            release(b)

        def quant_c(s):
            nc.vector.quantize_mx(
                out=cq[s][:].rearrange("p g n -> p (g n)").bitcast(FP8X4),
                scales=cs[s][:].rearrange("p g n -> p (g n)"),
                in_=cg[s][:].rearrange("p g n j -> p (g n j)"),
            )

        def widen(out, g, t, f0, f1, eng):
            in_ = wi[g][t // 2][:, t % 2, f0:f1].bitcast(FP8)
            if eng == "S":
                nc.scalar.activation(out=out, in_=in_, func=COPY, scale=wisc[:, g, t : t + 1])
            else:
                nc.vector.tensor_scalar(out=out, in0=in_, scalar1=wisc[:, g, t : t + 1], scalar2=None, op0=MULT)

        def widen_half(t, h, eng):
            widen(wb0[h][:, t, :], 0, t, 512 * h, 512 * h + 512, eng)

        def widen_row(t):
            widen(wb1[:, t, :], 1, t, 0, F, "V")

        def lace(g, h):
            rows = wb0[h][:] if g == 0 else wb1[:, :, 512 * h : 512 * h + 512]
            nc.vector.tensor_copy(
                out=wg[g][h][:].rearrange("p (t m j) -> p m j t", t=4, j=4),
                in_=rows.rearrange("p j (m t) -> p m j t", t=4),
            )

        def quant_wi(g, h, t0=0, t1=4):
            nc.vector.quantize_mx(
                out=wq[g][h][:, 128 * t0 : 128 * t1].bitcast(FP8X4),
                scales=ws[g][h][:, 128 * t0 : 128 * t1],
                in_=wg[g][h][:, 512 * t0 : 512 * t1],
            )

        def m_pass(out, g, t, a, n0, n1):
            c = n0 // 512
            nc.tensor.matmul_mx(
                out=out,
                lhsT=wuq[g][t][:, 128 * a : 128 * a + 128].bitcast(FP8X4),
                lhsT_scale=wus[g][t][:, 128 * a : 128 * a + 128],
                rhs=w4[c][a][:, 2 * (n0 - 512 * c) : 2 * (n1 - 512 * c)].bitcast(FP4X4),
                rhs_scale=w_scale(a, n0, n1),
                start=(a == 0),
                stop=(a == 1),
            )

        def one_pass(g, u, b, t, a):
            m_pass(b[:, 128 * t : 128 * t + 128], g, t, a, 128 * u, 128 * u + 128)

        def unit_part(g, u, b, ts):
            for t in ts:
                for a in range(2):
                    one_pass(g, u, b, t, a)
            return b

        def unit(g, u):
            return unit_part(g, u, bank(), range(4))

        def drain_m(g, u, b, eng):
            copy_out(
                eng,
                mx[g][u // 4][:, 512 * (u % 4) : 512 * (u % 4) + 512].rearrange("p (n t) -> p n t", t=4),
                b[:].rearrange("p (t n) -> p n t", t=4),
            )
            release(b)

        def units(g, u0, u1, eng):
            for u in range(u0, u1):
                drain_m(g, u, unit(g, u), eng)

        def units_two(g, u0, u1):
            for u in range(u0, u1, 2):
                pair = [unit(g, u), unit(g, u + 1)]
                drain_m(g, u + 1, pair[1], "S")
                drain_m(g, u, pair[0], "S")

        def quant_m(g, u0, u1):
            nc.vector.quantize_mx(
                out=mq[g][:, 128 * u0 : 128 * u1].bitcast(FP8X4),
                scales=ms[g][:, 128 * u0 : 128 * u1],
                in_=mx[g][u0 // 4][:, 512 * (u0 % 4) : 512 * ((u1 - 1) % 4 + 1)],
            )

        def pair_bank(g, c, q, v):
            b = bank()
            n = 512 * c + 256 * q
            for e in range(2):
                for a in range(2):
                    m_pass(b[:, 256 * e : 256 * e + 256], g, 2 * v + e, a, n, n + 256)
            return b

        def drain_pair(park, q, v, b, eng):
            planes = park[:].rearrange("p (v r) n -> p v (r n)", v=2)
            copy_out(
                eng,
                planes[:, v, 512 * q : 512 * q + 512].rearrange("p (n e) -> p n e", e=2),
                b[:].rearrange("p (e n) -> p n e", e=2),
            )
            release(b)

        def pair_half(g, c, q, park, order=(0, 1), engs="SS"):
            both = [pair_bank(g, c, q, v) for v in range(2)]
            for v in order:
                drain_pair(park, q, v, both[v], engs[v])

        def join(g, c, park, q0, q1):
            nc.vector.tensor_copy(
                out=mx[g][c][:, 1024 * q0 : 1024 * q1].bitcast(F32).rearrange("p (n v) -> p n v", v=2),
                in_=park[:].rearrange("p t n -> p (t n)").bitcast(F32).rearrange("p (v n) -> p n v", v=2)[:, 256 * q0 : 256 * q1, :],
            )

        def hidden(s, h, v):
            b = bank()
            for e in range(2):
                t = 2 * v + e
                for g in range(2):
                    nc.tensor.matmul_mx(
                        out=b[:, HALF * e : HALF * e + HALF],
                        lhsT=wq[g][h][:, 128 * t : 128 * t + 128].bitcast(FP8X4),
                        lhsT_scale=ws[g][h][:, 128 * t : 128 * t + 128],
                        rhs=cq[s][:, g, :].bitcast(FP8X4),
                        rhs_scale=cs[s][:, g, :],
                        start=(g == 0),
                        stop=(g == 1),
                    )
            return b

        def squash(s, h, v, b):
            for e in range(2):
                t = 2 * v + e
                nc.scalar.activation(
                    out=th[s][h][:, t, :], in_=b[:, HALF * e : HALF * e + HALF], func=TANH, bias=bcol[:, h, t : t + 1]
                )
            release(b)

        def hiddens(s, h):
            pair = [hidden(s, h, v) for v in range(2)]
            for v in (0, 1):
                squash(s, h, v, pair[v])

        def gains(s, h):
            nc.vector.tensor_tensor(
                out=hg[s][h][:].rearrange("p (c i) t -> p c t i", i=2),
                in0=th[s][h][:].rearrange("p t (c i) -> p c t i", i=2),
                in1=gcol[:, h, :].unsqueeze(1).unsqueeze(3).to_broadcast([P, HALF // 2, 4, 2]),
                op=MULT,
            )

        def quant_h(s, h):
            nc.vector.quantize_mx(
                out=hq[s][h][:].bitcast(FP8X4), scales=hs[s][h][:], in_=hg[s][h][:].rearrange("p n j -> p (n j)")
            )

        def final(i, n0, n1):
            b = bank()
            for g in range(2):
                nc.tensor.matmul_mx(
                    out=b[:, 0 : n1 - n0],
                    lhsT=hq[i // 2][g][:, 128 * (i % 2) : 128 * (i % 2) + 128].bitcast(FP8X4),
                    lhsT_scale=hs[i // 2][g][:, 128 * (i % 2) : 128 * (i % 2) + 128],
                    rhs=mq[g][:, n0:n1].bitcast(FP8X4),
                    rhs_scale=ms[g][:, n0:n1],
                    start=(g == 0),
                    stop=(g == 1),
                )
            return b

        def store(i, n0, y):
            nc.sync.dma_start(out=outs[n0 // 1024][i // 2][i % 2][:, n0 % 1024 : n0 % 1024 + 512], in_=y[:])

        def drain_y(i, n0, b, eng):
            y = yst.tile([P, 512], F32, name="y", tag="y", align_bytes=64)
            copy_out(eng, y[:], b[:])
            release(b)
            store(i, n0, y)

        def out_tile(i, n0, eng):
            drain_y(i, n0, final(i, n0, n0 + 512), eng)

        def finals_last(s, c):
            done = [final(2 * s + i, 512 * c, 512 * c + 512) for i in range(2)]
            for i in (1, 0):
                drain_y(2 * s + i, 512 * c, done[i], "S")

        def out_twin(i, n0, engs):
            y = yst.tile([P, 512], F32, name="y", tag="y", align_bytes=64)
            for e in range(2):
                b = final(i, n0 + 256 * e, n0 + 256 * e + 256)
                copy_out(engs[e], y[:, 256 * e : 256 * e + 256], b[:, 0:256])
                release(b)
            store(i, n0, y)

        def finals(s, c, engs):
            for i in range(2):
                out_tile(2 * s + i, 512 * c, engs[i])

        for x in w4s:
            nc.vector.memset(x[:].rearrange("p a n -> p (a n)").bitcast(I32), 0)
        nc.vector.tensor_copy(out=ident[:], in_=ident_bf[:])
        for t in range(4):
            load_wu(0, t)
        load_w4s(0)
        load_w4_pass(0, 0)
        load_w4_pass(0, 1)
        load_wi(0, 0, 2)
        load_wisc()
        load_wi(0, 2, 4)
        load_w4(1)
        load_w4s(1)
        load_w4(2)
        for t in range(4):
            load_wu(1, t)
        load_wi(1, 0, 2)
        load_wi(1, 2, 4)
        load_w4(3)
        for r in range(4):
            load_c(r)
        nc.sync.dma_start(out=bcol[:], in_=bias.rearrange("(g p t) -> p g t", p=P, t=4))
        nc.sync.dma_start(out=gcol[:], in_=gain.rearrange("(g p t) -> p g t", p=P, t=4))

        drain_plain(0, 0, turn_plain(0, 0), "S")
        drain_plain(0, 1, turn_plain(0, 1), "V")
        drain_plain(1, 0, turn_plain(1, 0), "S")
        drain_plain(1, 1, turn_plain(1, 1), "V")
        quant_wu(0, 0)
        for a in range(2):
            drain_plain(2, a, turn_plain(2, a), "S")
        quant_wu(0, 1)
        drain_plain(3, 0, turn_plain(3, 0), "V")
        drain_plain(3, 1, turn_plain(3, 1), "S")
        quant_wu(0, 2)
        quant_wu(0, 3)
        for t in (0, 2, 3):
            widen_half(t, 0, "V")
        widen_half(0, 1, "V")
        widen_half(1, 0, "S")
        for t in (1, 2, 3):
            widen_half(t, 1, "S")
        first = []
        for u in range(4):
            b = bank()
            first.append(b)
        for a in range(2):
            for u in range(4):
                one_pass(0, u, first[u], 0, a)
        for t in range(1, 4):
            for u in range(4):
                unit_part(0, u, first[u], [t])
        for u in (1, 0, 3, 2):
            drain_m(0, u, first[u], "S")
        lace(0, 0)
        units_two(0, 4, 8)
        lace(0, 1)
        take[0] = 1
        held = unit(0, 8)
        units(0, 9, 10, "S")
        pair_half(0, 2, 1, wb0[0], (1, 0))
        parts = [split(wu_raw[1][t]) for t in range(4)]
        drain_m(0, 8, held, "V")
        turned = [turn_split(x) for x in parts]
        for t in (1, 0, 3, 2):
            drain_wu(1, t, turned[t], "S")
        for t in range(4):
            widen_row(t)
        for q in range(2):
            pair_half(0, 3, q, wb0[1], (1, 0))
        parts = [split(craw[r]) for r in range(4)]
        for t in range(4):
            quant_wu(1, t)
        turned = [turn_split(x) for x in parts]
        for r in (1, 0, 3, 2):
            drain_c(r, turned[r], "S")
        lace(1, 0)
        lace(1, 1)
        units_two(1, 0, 6)
        units(1, 6, 7, "S")
        held = [unit(1, u) for u in (7, 8)]
        quant_wi(0, 0)
        quant_wi(1, 0)
        quant_c(0)
        quant_wi(0, 1)
        quant_wi(1, 1)
        hiddens(0, 0)
        quant_c(1)
        quant_m(0, 0, 4)
        hiddens(0, 1)
        quant_m(1, 0, 4)
        for u in (8, 7):
            drain_m(1, u, held[u - 7], "V")
        join(0, 2, wb0[0], 1, 2)
        gains(0, 0)
        take[0] = 2
        units_two(1, 9, 11)
        units(1, 11, 12, "S")
        gains(0, 1)
        quant_h(0, 0)
        quant_h(0, 1)
        quant_m(0, 4, 8)
        hiddens(1, 0)
        quant_m(1, 4, 8)
        hiddens(1, 1)
        quant_m(0, 8, 12)
        gains(1, 0)
        finals_last(0, 0)
        held = unit(1, 12)
        quant_m(1, 8, 12)
        gains(1, 1)
        quant_h(1, 0)
        quant_h(1, 1)
        finals_last(0, 1)
        drain_m(1, 12, held, "S")
        held = unit(1, 13)
        join(0, 3, wb0[1], 0, 2)
        finals(0, 2, "SV")
        drain_m(1, 13, held, "S")
        quant_m(0, 12, 16)
        held = unit(1, 14)
        finals(1, 0, "SS")
        drain_m(1, 14, held, "V")
        out_tile(2, 512, "S")
        quant_m(1, 12, 14)
        units(1, 15, 16, "V")
        out_twin(3, 512, "SS")
        quant_m(1, 14, 16)
        out_twin(2, 1024, "SS")
        out_twin(3, 1024, "VS")
        for i in range(4):
            out_twin(i, 1536, "VS")
